import numpy as np
import ml_dtypes


def mxq(x, axis, fmt="e4m3"):
    dtype, down = {"e4m3": (ml_dtypes.float8_e4m3fn, 7), "e5m2": (ml_dtypes.float8_e5m2, 14)}[fmt]
    v = np.moveaxis(np.asarray(x, np.float32).astype(ml_dtypes.bfloat16).astype(np.float64), axis, -1)
    blocks = v.reshape(v.shape[:-1] + (-1, 32))
    amax = np.abs(blocks).max(-1, keepdims=True)
    byte = np.maximum(np.where(amax > 0, np.frexp(amax)[1] - 1 + 127, 0) - down, 1)
    scale = np.exp2(byte - 127.0)
    codes = (blocks / scale).astype(np.float32).astype(dtype).astype(np.float64)
    return np.moveaxis((codes * scale).reshape(v.shape), -1, axis)


WIDE = False


def mx_kscale(k):
    if not WIDE:
        return np.ones(k)
    levels = np.array([10, -10, 5, -5, 0])
    if k % 512:
        return np.exp2(np.random.permutation(np.resize(levels, k // 32))).repeat(32)
    a = np.empty((k // 512, 16))
    for p in range(k // 512):
        a[p, :8] = np.random.permutation(np.resize(levels, 8))
        for g in range(8):
            far = levels[np.abs(levels - a[p, g]) >= 10]
            a[p, g + 8] = far[np.random.randint(len(far))]
    return np.exp2(a.ravel()).repeat(32)


BF16 = ml_dtypes.bfloat16


def bf(x):
    return np.asarray(x, np.float32).astype(BF16)


def f64(x):
    return np.asarray(x).astype(np.float64)


B, N, E, K, D = 4, 1024, 1024, 256, 1024

EPS = 1e-5


def softmax_last(v):
    e = np.exp(v - np.max(v, axis=-1, keepdims=True))
    return e / np.sum(e, axis=-1, keepdims=True)


def soft_assign(y, w, b):
    logits = (mxq(y, 2, "e4m3") @ mxq(w, 0, "e4m3")) + b
    return softmax_last(logits)


def rms_intra_norm(v):
    mean_sq = np.mean(v * v, axis=-1, keepdims=True)
    return v / np.sqrt(mean_sq + EPS)


def draw0():
    s, u = mx_kscale(E), mx_kscale(N)
    return {"y": bf(np.random.standard_normal((B, N, E)) * s),
            "w": bf(np.random.standard_normal((E, K)) * (1.5 / np.sqrt(E)) / s[:, None]),
            "b": bf(np.random.standard_normal(K) * 0.5),
            "t": bf(np.random.standard_normal(N) * 0.25 * u),
            "x": bf(np.random.standard_normal((B, N, D)) * (0.016 * K / np.sqrt(N)) / u[:, None]),
            "c": bf(np.random.standard_normal((K, D)) * (0.012 * K / N))}


def core(y, w, b, t, x, c):
    a = soft_assign(f64(y), f64(w), f64(b))
    r = a * f64(t)[None, :, None]
    rq = mxq(r, 1, "e4m3")
    xq = mxq(f64(x), 1, "e4m3")
    sums = rq.transpose(0, 2, 1) @ xq
    m = np.sum(a, axis=1)
    v = sums - m[:, :, None] * f64(c)[None, :, :]
    return rms_intra_norm(v)


def e4m3fn_bytes(y):
    return np.clip(np.asarray(y, np.float64), -448.0, 448.0).astype(np.float32).astype(ml_dtypes.float8_e4m3fn).view(np.uint8)


def e4m3fn_values(b):
    return np.asarray(b, np.uint8).view(ml_dtypes.float8_e4m3fn).astype(np.float64)


def setup_inputs():
    d = draw0()
    x0 = np.asarray(d['y']).astype(np.float64)
    s = (np.max(np.abs(x0), axis=(0, 1), keepdims=True) / 448.0).astype(np.float32)
    out = {}
    for k, v in d.items():
        if k == 'y':
            out['y_bytes'] = e4m3fn_bytes(x0 / s.astype(np.float64))
            out['y_scale'] = s
        else:
            out[k] = v
    return out


def reference(y_bytes, y_scale, w, b, t, x, c):
    return core(e4m3fn_values(y_bytes) * y_scale.astype(np.float64), w, b, t, x, c)

@@ -1,0 +1,372 @@
+from contextlib import ExitStack
+
+import concourse.mybir as mybir
+from concourse.masks import make_identity
+
+B, N, E, K, D = 4, 1024, 1024, 256, 1024
+EPS = 1e-5
+FLOPS = 2 * B * N * E * K + 2 * B * N * K * D
+
+F32 = mybir.dt.float32
+BF16 = mybir.dt.bfloat16
+U32 = mybir.dt.uint32
+U8 = mybir.dt.uint8
+FP8 = mybir.dt.float8_e4m3fn
+FP8X4 = mybir.dt.float8_e4m3fn_x4
+ALU = mybir.AluOpType
+ACT = mybir.ActivationFunctionType
+AXIS = mybir.AxisListType
+
+P = 128
+PACK = 4
+PASS = P * PACK
+BANK = 512
+E_PASSES = E // PASS
+N_PASSES = N // PASS
+HALVES = K // P
+UNITS = B * N_PASSES
+XI_PIECES = 8
+LAG = 5
+AHEAD = 4
+
+
+def tile_crossmodalreweightedvlad_kernel(tc, y_bytes, y_scale, w, b, t, x, c, out):
+    nc = tc.nc
+    with ExitStack() as ctx:
+        const = ctx.enter_context(tc.tile_pool(name="const", bufs=1))
+        work = ctx.enter_context(tc.tile_pool(name="work", bufs=2))
+        psum = ctx.enter_context(tc.psum_pool(name="psum", bufs=2))
+        ctx.enter_context(tc.manual_schedule())
+
+        ident = const.tile([P, P], F32, name="ident")
+        make_identity(nc, ident[:])
+        minus_half = const.tile([P, 1], F32, name="minus_half")
+        nc.gpsimd.memset(minus_half[:], -0.5)
+        warm_in = const.tile([P, 1], F32, name="warm_in")
+        warm_out = const.tile([P, 1], F32, name="warm_out")
+        nc.vector.memset(warm_in[:], 0.0)
+        nc.scalar.activation(out=warm_out[:], in_=warm_in[:], func=ACT.Exp)
+
+        scale_rows = const.tile([P, E], F32, name="scale_rows")
+        w_raw = const.tile([P, E_PASSES, PACK, K], BF16, name="w_raw")
+        w_grouped = const.tile([P, E_PASSES, K, PACK], BF16, name="w_grouped", align_bytes=64)
+        w_codes = const.tile([P, E_PASSES, K], U32, name="w_codes", align_bytes=64)
+        w_scales = const.tile([P, E_PASSES, K], U8, name="w_scales", align_bytes=64)
+        b_cols = const.tile([P, HALVES], BF16, name="b_cols")
+        neg_b = const.tile([P, HALVES], F32, name="neg_b")
+        t_cols = const.tile([P, N_PASSES, PACK], BF16, name="t_cols")
+        c_rows = const.tile([P, HALVES, D], BF16, name="c_rows")
+
+        y_raw, x_raw, y_scaled, y_turned, y_grouped, y_q = {}, {}, {}, {}, {}, {}
+        lt, zt, zb, neg_max, expd, sums, recip, factor = {}, {}, {}, {}, {}, {}, {}, {}
+        r_grouped, r_q, x_grouped, x_q, mass, s_bank, neg_v, mean_sq, rstd = {}, {}, {}, {}, {}, {}, {}, {}, {}
+
+        def load_y(u, slots):
+            i, g = divmod(u, N_PASSES)
+            rows = work.tile([P, len(slots), E], U8, name="y_raw", bufs=AHEAD + 2)
+            src = y_bytes[i, g * PASS:(g + 1) * PASS, :].rearrange("(p s) e -> p s e", s=PACK)
+            nc.sync.dma_start(out=rows[:], in_=src[:, slots[0]:slots[-1] + 1, :])
+            for s in slots:
+                y_raw[u, s] = rows[:, s - slots[0], :]
+
+        def load_x(u):
+            i, g = divmod(u, N_PASSES)
+            x_raw[u] = work.tile([P, PACK, D], BF16, name="x_raw", bufs=AHEAD)
+            nc.sync.dma_start(out=x_raw[u][:], in_=x[i, g * PASS:(g + 1) * PASS, :].rearrange("(p t) d -> p t d", t=PACK))
+
+        def load_unit(u):
+            load_y(u, range(PACK))
+            load_x(u)
+
+        def quantize(name, src, width, bufs):
+            codes = work.tile([P, width], U32, name=name + "_codes", bufs=bufs, align_bytes=64)
+            scales = work.tile([P, width], U8, name=name + "_scales", bufs=bufs, align_bytes=64)
+            nc.vector.quantize_mx(out=codes[:].bitcast(FP8X4), scales=scales[:], in_=src)
+            return codes, scales
+
+        def scale_y(u, s):
+            y_scaled[u, s] = work.tile([P, E], BF16, name="y_scaled", bufs=5)
+            nc.vector.tensor_tensor(out=y_scaled[u, s][:], in0=y_raw[u, s].bitcast(FP8),
+                                    in1=scale_rows[:], op=ALU.mult)
+
+        def turn_y(u, s):
+            words = y_scaled[u, s][:].bitcast(F32)
+            y_turned[u, s] = psum.tile([P, E_PASSES, 2, P], F32, name="y_turned", tag="turn")
+            for g in range(E_PASSES):
+                for pair in range(2):
+                    nc.tensor.transpose(y_turned[u, s][:, g, pair, :],
+                                        words[:, 2 * P * g + pair:2 * P * (g + 1):2], ident[:])
+
+        def empty_y(u, s):
+            if s == 0:
+                y_grouped[u] = work.tile([P, E_PASSES, PACK, 2 * P], F32, name="y_grouped", align_bytes=64)
+            nc.scalar.copy(out=y_grouped[u][:, :, s, :].rearrange("p g (n u) -> p g n u", u=2),
+                           in_=y_turned[u, s][:].rearrange("p g u n -> p g n u"))
+
+        def quantize_y(u):
+            y_q[u] = quantize("y", y_grouped[u][:].rearrange("p g s n -> p (g s n)").bitcast(BF16), E_PASSES * PASS, 2)
+
+        def logits(u):
+            codes, scales = y_q[u]
+            for h in range(HALVES):
+                lt[u, h] = psum.tile([P, PASS], F32, name="lt", tag="logit")
+                cols = slice(h * P, (h + 1) * P)
+                for g in range(E_PASSES):
+                    toks = slice(g * PASS, (g + 1) * PASS)
+                    nc.tensor.matmul_mx(out=lt[u, h][:], lhsT=w_codes[:, g, cols].bitcast(FP8X4),
+                                        lhsT_scale=w_scales[:, g, cols], rhs=codes[:, toks].bitcast(FP8X4),
+                                        rhs_scale=scales[:, toks], start=(g == 0), stop=(g == E_PASSES - 1))
+
+        def add_bias(u, h):
+            zt[u, h] = work.tile([P, PASS], F32, name="zt", bufs=2)
+            nc.scalar.activation(out=zt[u, h][:], in_=lt[u, h][:], func=ACT.Identity,
+                                 bias=neg_b[:, h:h + 1], scale=-1.0)
+
+        def turn_logits(u):
+            for half in range(2):
+                zb[u, half] = psum.tile([P, 2, K], F32, name="zb", tag="zb")
+                for s2 in range(2):
+                    s = 2 * half + s2
+                    for h in range(HALVES):
+                        nc.tensor.transpose(zb[u, half][:, s2, h * P:(h + 1) * P], zt[u, h][:, s * P:(s + 1) * P], ident[:])
+
+        def row_max(u, half):
+            neg_max[u, half] = work.tile([P, 2], F32, name="neg_max", bufs=4)
+            nc.vector.tensor_reduce(out=neg_max[u, half][:], in_=zb[u, half][:], axis=AXIS.X, op=ALU.min)
+
+        def exponentiate(u, half):
+            if half == 0:
+                expd[u] = work.tile([P, PACK, K], F32, name="expd")
+                sums[u] = work.tile([P, PACK], F32, name="sums")
+            for s2 in range(2):
+                s = 2 * half + s2
+                nc.scalar.activation(out=expd[u][:, s, :], in_=zb[u, half][:, s2, :], func=ACT.Exp,
+                                     bias=neg_max[u, half][:, s2:s2 + 1], scale=-1.0, accum_out=sums[u][:, s:s + 1])
+
+        def invert_sums(u):
+            recip[u] = work.tile([P, PACK], F32, name="recip")
+            nc.vector.reciprocal(out=recip[u][:], in_=sums[u][:])
+
+        def row_factor(u):
+            factor[u] = work.tile([P, PACK], F32, name="factor")
+            nc.vector.tensor_tensor(out=factor[u][:], in0=recip[u][:], in1=t_cols[:, u % N_PASSES, :], op=ALU.mult)
+
+        def reweight(u):
+            r_grouped[u] = work.tile([P, K, PACK], BF16, name="r_grouped", align_bytes=64)
+            nc.vector.tensor_tensor(out=r_grouped[u][:].rearrange("p (c i) s -> p c s i", i=2),
+                                    in0=expd[u][:].rearrange("p s (c i) -> p c s i", i=2),
+                                    in1=factor[u][:].unsqueeze(1).unsqueeze(3).to_broadcast([P, K // 2, PACK, 2]), op=ALU.mult)
+
+        def quantize_r(u):
+            r_q[u] = quantize("r", r_grouped[u][:].rearrange("p k s -> p (k s)"), K, LAG)
+
+        def group_x(u, piece, copy=nc.scalar.copy):
+            if piece == 0:
+                x_grouped[u] = work.tile([P, D, PACK], BF16, name="x_grouped", align_bytes=64)
+            cols = slice(piece * D // XI_PIECES, (piece + 1) * D // XI_PIECES)
+            copy(out=x_grouped[u][:, cols, :].rearrange("p (c i) s -> p c s i", i=4),
+                 in_=x_raw[u][:, :, cols].rearrange("p s (c i) -> p c s i", i=4))
+
+        def quantize_x(u):
+            x_q[u] = quantize("x", x_grouped[u][:].rearrange("p d s -> p (d s)"), D, LAG + 1)
+
+        def mass_matmul(u):
+            mass[u, "bank"] = psum.tile([P, HALVES], F32, name="mass_bank", tag="logit")
+            for h in range(HALVES):
+                for s in range(PACK):
+                    nc.tensor.matmul(mass[u, "bank"][:, h:h + 1], lhsT=expd[u][:, s, h * P:(h + 1) * P],
+                                     rhs=recip[u][:, s:s + 1], start=(s == 0), stop=(s == PACK - 1))
+
+        def mass_collect(u):
+            mass[u] = work.tile([P, HALVES], F32, name="mass", bufs=UNITS)
+            if u % N_PASSES == 0:
+                nc.vector.tensor_scalar(out=mass[u][:], in0=mass[u, "bank"][:], scalar1=-1.0, scalar2=None, op0=ALU.mult)
+            else:
+                nc.vector.tensor_tensor(out=mass[u][:], in0=mass[u - 1][:], in1=mass[u, "bank"][:], op=ALU.subtract)
+
+        def pool_matmul(q, tag, passes):
+            i, h = divmod(q, HALVES)
+            cols = slice(h * P, (h + 1) * P)
+            for dh in range(D // BANK):
+                if passes[0] == 0:
+                    s_bank[q, dh] = psum.tile([P, BANK], F32, name="s_bank", tag=tag)
+                feats = slice(dh * BANK, (dh + 1) * BANK)
+                for g in passes:
+                    r_codes, r_scales = r_q[N_PASSES * i + g]
+                    x_codes, x_scales = x_q[N_PASSES * i + g]
+                    nc.tensor.matmul_mx(out=s_bank[q, dh][:], lhsT=r_codes[:, cols].bitcast(FP8X4),
+                                        lhsT_scale=r_scales[:, cols], rhs=x_codes[:, feats].bitcast(FP8X4),
+                                        rhs_scale=x_scales[:, feats], start=(g == 0), stop=(g == N_PASSES - 1))
+
+        def centre(q, dh):
+            i, h = divmod(q, HALVES)
+            if dh == 0:
+                neg_v[q] = work.tile([P, D], F32, name="neg_v", bufs=4)
+            total = mass[N_PASSES * i + N_PASSES - 1]
+            feats = slice(dh * BANK, (dh + 1) * BANK)
+            nc.vector.scalar_tensor_tensor(out=neg_v[q][:, feats], in0=c_rows[:, h, feats], scalar=total[:, h:h + 1],
+                                           in1=s_bank[q, dh][:], op0=ALU.mult, op1=ALU.add)
+
+        def mean_square(q):
+            squares = work.tile([P, D], BF16, name="squares", bufs=2)
+            mean_sq[q] = work.tile([P, 1], F32, name="mean_sq", bufs=4)
+            nc.scalar.activation(out=squares[:], in_=neg_v[q][:], func=ACT.Square, scale=D ** -0.5,
+                                 accum_out=mean_sq[q][:])
+
+        def inverse_root_pow(q):
+            shifted = work.tile([P, 1], F32, name="shifted")
+            rstd[q] = work.tile([P, 1], F32, name="rstd", bufs=4)
+            nc.gpsimd.tensor_scalar(out=shifted[:], in0=mean_sq[q][:], scalar1=EPS, scalar2=1.0, op0=ALU.add, op1=ALU.mult)
+            nc.gpsimd.tensor_tensor(out=rstd[q][:], in0=shifted[:], in1=minus_half[:], op=ALU.pow)
+
+        def root(q):
+            rms[q] = work.tile([P, 1], F32, name="rms", bufs=4)
+            nc.scalar.activation(out=rms[q][:], in_=mean_sq[q][:], func=ACT.Sqrt, bias=EPS)
+
+        def invert_root(q):
+            rstd[q] = work.tile([P, 1], F32, name="rstd_tail", bufs=4)
+            nc.vector.reciprocal(out=rstd[q][:], in_=rms[q][:])
+
+        def normalise(q, parts=1, on_scalar=False):
+            i, h = divmod(q, HALVES)
+            for part in range(parts):
+                feats = slice(part * D // parts, (part + 1) * D // parts)
+                result = work.tile([P, D // parts], F32, name="result", bufs=6)
+                if on_scalar:
+                    nc.scalar.activation(out=result[:], in_=neg_v[q][:, feats], func=ACT.Copy, scale=rstd[q][:])
+                else:
+                    nc.vector.tensor_scalar(out=result[:], in0=neg_v[q][:, feats], scalar1=rstd[q][:], scalar2=None,
+                                            op0=ALU.mult)
+                nc.sync.dma_start(out=out[i].rearrange("(p h) d -> p h d", h=HALVES)[:, h, feats], in_=result[:])
+
+        rms = {}
+        both = list(range(N_PASSES))
+
+        load_y(0, [0])
+        nc.sync.dma_start(out=scale_rows[:], in_=y_scale.rearrange("a o e -> (a o e)").partition_broadcast(P))
+        load_y(0, [1, 2, 3])
+        nc.sync.dma_start(out=w_raw[:], in_=w.rearrange("(g p t) k -> p g t k", p=P, t=PACK))
+        load_x(0)
+        nc.sync.dma_start(out=b_cols[:], in_=b.rearrange("(p h) -> p h", h=HALVES))
+        nc.sync.dma_start(out=t_cols[:], in_=t.rearrange("(g p s) -> p g s", p=P, s=PACK))
+        load_unit(1)
+        nc.sync.dma_start(out=c_rows[:], in_=c.rearrange("(p h) d -> p h d", h=HALVES))
+        for u in range(2, AHEAD):
+            load_unit(u)
+        for g in range(E_PASSES):
+            nc.scalar.copy(out=w_grouped[:, g, :, :].rearrange("p (h m) t -> p h m t", h=HALVES),
+                           in_=w_raw[:, g, :, :].rearrange("p t (m h) -> p h m t", h=HALVES))
+
+
+        def quantize_w():
+            nc.vector.quantize_mx(out=w_codes[:].rearrange("p g k -> p (g k)").bitcast(FP8X4),
+                                  scales=w_scales[:].rearrange("p g k -> p (g k)"),
+                                  in_=w_grouped[:].rearrange("p g k t -> p (g k t)"))
+
+        def when(u, step, *args):
+            if 0 <= u < UNITS:
+                step(u, *args)
+
+        for s in range(PACK):
+            scale_y(0, s)
+            turn_y(0, s)
+            empty_y(0, s)
+        quantize_w()
+        nc.vector.tensor_scalar(out=neg_b[:], in0=b_cols[:], scalar1=-1.0, scalar2=None, op0=ALU.mult)
+        for piece in range(3):
+            group_x(0, piece)
+
+        for j in range(1, UNITS + 1):
+            q = j - LAG
+            if j > 1:
+                quantize_y(j - 1)
+            when(j, scale_y, 0)
+            when(j - 3, quantize_r)
+            when(j - 3, mass_collect)
+            when(j, scale_y, 1)
+            if j == 1:
+                quantize_y(j - 1)
+            logits(j - 1)
+            on_vector = 5 if j == 1 else (1 if j < LAG - 1 else 0)
+            for piece in range(3, XI_PIECES - on_vector):
+                group_x(j - 1, piece)
+            when(j, turn_y, 0)
+            when(j, turn_y, 1)
+            add_bias(j - 1, 0)
+            add_bias(j - 1, 1)
+            when(j - 2, row_max, 0)
+            when(j - 2, row_max, 1)
+            when(j, group_x, 0)
+            when(j - 2, exponentiate, 0)
+            when(j - 2, exponentiate, 1)
+            when(j, scale_y, 2)
+            when(j, scale_y, 3)
+            for piece in range(XI_PIECES - on_vector, XI_PIECES):
+                group_x(j - 1, piece, nc.vector.tensor_copy)
+            when(j, empty_y, 0)
+            when(j, empty_y, 1)
+            turn_logits(j - 1)
+            when(j, turn_y, 2)
+            when(j, turn_y, 3)
+            when(j, group_x, 1)
+            when(q, centre, 0)
+            when(q, centre, 1)
+            when(q, mean_square)
+            when(q, inverse_root_pow)
+            when(j, empty_y, 2)
+            when(j, empty_y, 3)
+            when(j, group_x, 2)
+            when(q + 1, pool_matmul, "s", both)
+            when(j - 2, invert_sums)
+            when(j - 2, mass_matmul)
+            quantize_x(j - 1)
+            when(j - 2, row_factor)
+            when(q - 1, normalise, 1, j == UNITS)
+            when(j - 2, reweight)
+            when(j + AHEAD - 1, load_unit)
+
+        last = UNITS - 1
+        q = UNITS + 1 - LAG
+        assert q == UNITS - 4
+        row_max(last, 0)
+        row_max(last, 1)
+        mass_collect(last - 1)
+        quantize_r(last - 1)
+        exponentiate(last, 0)
+        exponentiate(last, 1)
+        pool_matmul(q + 1, "turn", both)
+        centre(q, 0)
+        centre(q, 1)
+        pool_matmul(UNITS - 2, "s", [0])
+        mean_square(q)
+        centre(q + 1, 0)
+        invert_sums(last)
+        mass_matmul(last)
+        centre(q + 1, 1)
+        row_factor(last)
+        normalise(q - 1)
+        pool_matmul(UNITS - 1, "turn", [0])
+        root(q)
+        mean_square(q + 1)
+        root(q + 1)
+        reweight(last)
+        mass_collect(last)
+        quantize_r(last)
+        pool_matmul(UNITS - 2, "s", [1])
+        pool_matmul(UNITS - 1, "turn", [1])
+        invert_root(q)
+        centre(UNITS - 2, 0)
+        centre(UNITS - 2, 1)
+        mean_square(UNITS - 2)
+        centre(UNITS - 1, 0)
+        centre(UNITS - 1, 1)
+        invert_root(q + 1)
+        normalise(q)
+        normalise(q + 1)
+        root(UNITS - 2)
+        mean_square(UNITS - 1)
+        invert_root(UNITS - 2)
+        root(UNITS - 1)
+        normalise(UNITS - 2)
+        invert_root(UNITS - 1)
+        normalise(UNITS - 1, 2)

@@ -25,9 +25,10 @@ E_PASSES = E // PASS
 N_PASSES = N // PASS
 HALVES = K // P
 UNITS = B * N_PASSES
-XI_PIECES = 8
+SHARES = [0, 512, 512, 128, 0, 0, 0, 0]
 LAG = 5
 AHEAD = 4
+MASS_COLS = 64
 
 
 def tile_crossmodalreweightedvlad_kernel(tc, y_bytes, y_scale, w, b, t, x, c, out):
@@ -47,7 +48,7 @@ def tile_crossmodalreweightedvlad_kernel(tc, y_bytes, y_scale, w, b, t, x, c, ou
         nc.vector.memset(warm_in[:], 0.0)
         nc.scalar.activation(out=warm_out[:], in_=warm_in[:], func=ACT.Exp)
 
-        scale_rows = const.tile([P, E], F32, name="scale_rows")
+        scale_rows = const.tile([P, 2 * E], F32, name="scale_rows")
         w_raw = const.tile([P, E_PASSES, PACK, K], BF16, name="w_raw")
         w_grouped = const.tile([P, E_PASSES, K, PACK], BF16, name="w_grouped", align_bytes=64)
         w_codes = const.tile([P, E_PASSES, K], U32, name="w_codes", align_bytes=64)
@@ -61,13 +62,13 @@ def tile_crossmodalreweightedvlad_kernel(tc, y_bytes, y_scale, w, b, t, x, c, ou
         lt, zt, zb, neg_max, expd, sums, recip, factor = {}, {}, {}, {}, {}, {}, {}, {}
         r_grouped, r_q, x_grouped, x_q, mass, s_bank, neg_v, mean_sq, rstd = {}, {}, {}, {}, {}, {}, {}, {}, {}
 
-        def load_y(u, slots):
+        def load_y(u, halves):
             i, g = divmod(u, N_PASSES)
-            rows = work.tile([P, len(slots), E], U8, name="y_raw", bufs=AHEAD + 2)
-            src = y_bytes[i, g * PASS:(g + 1) * PASS, :].rearrange("(p s) e -> p s e", s=PACK)
-            nc.sync.dma_start(out=rows[:], in_=src[:, slots[0]:slots[-1] + 1, :])
-            for s in slots:
-                y_raw[u, s] = rows[:, s - slots[0], :]
+            rows = work.tile([P, len(halves) * 2 * E], U8, name="y_raw", bufs=AHEAD + 2)
+            src = y_bytes[i, g * PASS:(g + 1) * PASS, :].rearrange("(p s) e -> p (s e)", s=PACK)
+            nc.sync.dma_start(out=rows[:], in_=src[:, halves[0] * 2 * E:(halves[-1] + 1) * 2 * E])
+            for n, half in enumerate(halves):
+                y_raw[u, half] = rows[:, n * 2 * E:(n + 1) * 2 * E]
 
         def load_x(u):
             i, g = divmod(u, N_PASSES)
@@ -75,7 +76,7 @@ def tile_crossmodalreweightedvlad_kernel(tc, y_bytes, y_scale, w, b, t, x, c, ou
             nc.sync.dma_start(out=x_raw[u][:], in_=x[i, g * PASS:(g + 1) * PASS, :].rearrange("(p t) d -> p t d", t=PACK))
 
         def load_unit(u):
-            load_y(u, range(PACK))
+            load_y(u, [0, 1])
             load_x(u)
 
         def quantize(name, src, width, bufs):
@@ -84,13 +85,13 @@ def tile_crossmodalreweightedvlad_kernel(tc, y_bytes, y_scale, w, b, t, x, c, ou
             nc.vector.quantize_mx(out=codes[:].bitcast(FP8X4), scales=scales[:], in_=src)
             return codes, scales
 
-        def scale_y(u, s):
-            y_scaled[u, s] = work.tile([P, E], BF16, name="y_scaled", bufs=5)
-            nc.vector.tensor_tensor(out=y_scaled[u, s][:], in0=y_raw[u, s].bitcast(FP8),
+        def scale_y(u, half):
+            y_scaled[u, half] = work.tile([P, 2 * E], BF16, name="y_scaled", bufs=3)
+            nc.vector.tensor_tensor(out=y_scaled[u, half][:], in0=y_raw[u, half].bitcast(FP8),
                                     in1=scale_rows[:], op=ALU.mult)
 
         def turn_y(u, s):
-            words = y_scaled[u, s][:].bitcast(F32)
+            words = y_scaled[u, s // 2][:].bitcast(F32)[:, (s % 2) * E // 2:(s % 2 + 1) * E // 2]
             y_turned[u, s] = psum.tile([P, E_PASSES, 2, P], F32, name="y_turned", tag="turn")
             for g in range(E_PASSES):
                 for pair in range(2):
@@ -160,29 +161,45 @@ def tile_crossmodalreweightedvlad_kernel(tc, y_bytes, y_scale, w, b, t, x, c, ou
         def quantize_r(u):
             r_q[u] = quantize("r", r_grouped[u][:].rearrange("p k s -> p (k s)"), K, LAG)
 
-        def group_x(u, piece, copy=nc.scalar.copy):
-            if piece == 0:
-                x_grouped[u] = work.tile([P, D, PACK], BF16, name="x_grouped", align_bytes=64)
-            cols = slice(piece * D // XI_PIECES, (piece + 1) * D // XI_PIECES)
-            copy(out=x_grouped[u][:, cols, :].rearrange("p (c i) s -> p c s i", i=4),
-                 in_=x_raw[u][:, :, cols].rearrange("p s (c i) -> p c s i", i=4))
+        def share(u):
+            return SHARES[u]
+
+        def group_x_half(u, half, copy=nc.scalar.copy):
+            mid = (share(u) + D) // 2
+            group_x(u, *((share(u), mid), (mid, D))[half], copy)
+
+        def open_x(u):
+            x_grouped[u] = work.tile([P, D, PACK], BF16, name="x_grouped", align_bytes=64)
+
+        def x_views(u, lo, hi):
+            return (x_grouped[u][:, lo:hi, :].rearrange("p (c i) s -> p c s i", i=4),
+                    x_raw[u][:, :, lo:hi].rearrange("p s (c i) -> p c s i", i=4))
+
+        def group_x(u, lo, hi, copy=nc.scalar.copy):
+            dst, src = x_views(u, lo, hi)
+            copy(out=dst, in_=src)
+
+        def group_x_vector(u):
+            if share(u):
+                group_x(u, 0, share(u), nc.vector.tensor_copy)
 
         def quantize_x(u):
             x_q[u] = quantize("x", x_grouped[u][:].rearrange("p d s -> p (d s)"), D, LAG + 1)
 
-        def mass_matmul(u):
-            mass[u, "bank"] = psum.tile([P, HALVES], F32, name="mass_bank", tag="logit")
+        def mass_matmul(u, tag):
+            mass_bank[u] = psum.tile([P, HALVES, MASS_COLS], F32, name="mass_bank", tag=tag)
             for h in range(HALVES):
                 for s in range(PACK):
-                    nc.tensor.matmul(mass[u, "bank"][:, h:h + 1], lhsT=expd[u][:, s, h * P:(h + 1) * P],
-                                     rhs=recip[u][:, s:s + 1], start=(s == 0), stop=(s == PACK - 1))
+                    nc.tensor.matmul(mass_bank[u][:, h, :], lhsT=expd[u][:, s, h * P:(h + 1) * P],
+                                     rhs=recip[u][:, s:s + 1].to_broadcast([P, MASS_COLS]),
+                                     start=(s == 0), stop=(s == PACK - 1))
 
         def mass_collect(u):
             mass[u] = work.tile([P, HALVES], F32, name="mass", bufs=UNITS)
             if u % N_PASSES == 0:
-                nc.vector.tensor_scalar(out=mass[u][:], in0=mass[u, "bank"][:], scalar1=-1.0, scalar2=None, op0=ALU.mult)
+                nc.vector.tensor_scalar(out=mass[u][:], in0=mass_bank[u][:, :, 0], scalar1=-1.0, scalar2=None, op0=ALU.mult)
             else:
-                nc.vector.tensor_tensor(out=mass[u][:], in0=mass[u - 1][:], in1=mass[u, "bank"][:], op=ALU.subtract)
+                nc.vector.tensor_tensor(out=mass[u][:], in0=mass[u - 1][:], in1=mass_bank[u][:, :, 0], op=ALU.subtract)
 
         def pool_matmul(q, tag, passes):
             i, h = divmod(q, HALVES)
@@ -201,10 +218,9 @@ def tile_crossmodalreweightedvlad_kernel(tc, y_bytes, y_scale, w, b, t, x, c, ou
         def centre(q, dh):
             i, h = divmod(q, HALVES)
             if dh == 0:
-                neg_v[q] = work.tile([P, D], F32, name="neg_v", bufs=4)
-            total = mass[N_PASSES * i + N_PASSES - 1]
+                neg_v[q] = work.tile([P, D], F32, name="neg_v", bufs=5)
             feats = slice(dh * BANK, (dh + 1) * BANK)
-            nc.vector.scalar_tensor_tensor(out=neg_v[q][:, feats], in0=c_rows[:, h, feats], scalar=total[:, h:h + 1],
+            nc.vector.scalar_tensor_tensor(out=neg_v[q][:, feats], in0=c_rows[:, h, feats], scalar=mass[N_PASSES * i + N_PASSES - 1][:, h:h + 1],
                                            in1=s_bank[q, dh][:], op0=ALU.mult, op1=ALU.add)
 
         def mean_square(q):
@@ -231,7 +247,7 @@ def tile_crossmodalreweightedvlad_kernel(tc, y_bytes, y_scale, w, b, t, x, c, ou
             i, h = divmod(q, HALVES)
             for part in range(parts):
                 feats = slice(part * D // parts, (part + 1) * D // parts)
-                result = work.tile([P, D // parts], F32, name="result", bufs=6)
+                result = work.tile([P, D // parts], F32, name="result", bufs=5)
                 if on_scalar:
                     nc.scalar.activation(out=result[:], in_=neg_v[q][:, feats], func=ACT.Copy, scale=rstd[q][:])
                 else:
@@ -239,24 +255,33 @@ def tile_crossmodalreweightedvlad_kernel(tc, y_bytes, y_scale, w, b, t, x, c, ou
                                             op0=ALU.mult)
                 nc.sync.dma_start(out=out[i].rearrange("(p h) d -> p h d", h=HALVES)[:, h, feats], in_=result[:])
 
-        rms = {}
+        rms, mass_bank = {}, {}
         both = list(range(N_PASSES))
 
-        load_y(0, [0])
-        nc.sync.dma_start(out=scale_rows[:], in_=y_scale.rearrange("a o e -> (a o e)").partition_broadcast(P))
-        load_y(0, [1, 2, 3])
+        per_part = E // P
+        scale_cols = const.tile([P, per_part], F32, name="scale_cols")
+        nc.sync.dma_start(out=scale_cols[:], in_=y_scale.rearrange("a o (p j) -> p (a o j)", p=P))
         nc.sync.dma_start(out=w_raw[:], in_=w.rearrange("(g p t) k -> p g t k", p=P, t=PACK))
+        load_y(0, [0])
         load_x(0)
+        load_y(0, [1])
         nc.sync.dma_start(out=b_cols[:], in_=b.rearrange("(p h) -> p h", h=HALVES))
         nc.sync.dma_start(out=t_cols[:], in_=t.rearrange("(g p s) -> p g s", p=P, s=PACK))
         load_unit(1)
         nc.sync.dma_start(out=c_rows[:], in_=c.rearrange("(p h) d -> p h d", h=HALVES))
         for u in range(2, AHEAD):
             load_unit(u)
+        for half in range(2):
+            spread = psum.tile([P, PACK, P], F32, name="spread", tag="zb")
+            for jj in range(PACK):
+                col = half * PACK + jj
+                nc.tensor.transpose(spread[:, jj, :], scale_cols[:, col:col + 1].to_broadcast([P, P]), ident[:])
+            nc.scalar.copy(out=scale_rows[:, :E].rearrange("q (p j) -> q p j", j=per_part)[:, :, half * PACK:(half + 1) * PACK],
+                           in_=spread[:].rearrange("q j p -> q p j"))
+        nc.scalar.copy(out=scale_rows[:, E:], in_=scale_rows[:, :E])
         for g in range(E_PASSES):
-            nc.scalar.copy(out=w_grouped[:, g, :, :].rearrange("p (h m) t -> p h m t", h=HALVES),
-                           in_=w_raw[:, g, :, :].rearrange("p t (m h) -> p h m t", h=HALVES))
-
+            nc.vector.tensor_copy(out=w_grouped[:, g, :, :].rearrange("p (h m) t -> p h m t", h=HALVES),
+                                  in_=w_raw[:, g, :, :].rearrange("p t (m h) -> p h m t", h=HALVES))
 
         def quantize_w():
             nc.vector.quantize_mx(out=w_codes[:].rearrange("p g k -> p (g k)").bitcast(FP8X4),
@@ -267,106 +292,143 @@ def tile_crossmodalreweightedvlad_kernel(tc, y_bytes, y_scale, w, b, t, x, c, ou
             if 0 <= u < UNITS:
                 step(u, *args)
 
-        for s in range(PACK):
-            scale_y(0, s)
-            turn_y(0, s)
-            empty_y(0, s)
         quantize_w()
+        scale_y(0, 0)
+        scale_y(0, 1)
         nc.vector.tensor_scalar(out=neg_b[:], in0=b_cols[:], scalar1=-1.0, scalar2=None, op0=ALU.mult)
-        for piece in range(3):
-            group_x(0, piece)
+        open_x(0)
+        group_x_half(0, 0)
+        turn_y(0, 0)
+        turn_y(0, 1)
+        empty_y(0, 0)
+        empty_y(0, 1)
+        turn_y(0, 2)
+        turn_y(0, 3)
+        empty_y(0, 2)
+        empty_y(0, 3)
+        group_x_half(0, 1)
 
-        for j in range(1, UNITS + 1):
+        for j in range(1, UNITS):
             q = j - LAG
             if j > 1:
                 quantize_y(j - 1)
-            when(j, scale_y, 0)
-            when(j - 3, quantize_r)
-            when(j - 3, mass_collect)
-            when(j, scale_y, 1)
+            when(j - 4, mass_collect)
+            when(j - 3, invert_sums)
+            scale_y(j, 0)
             if j == 1:
-                quantize_y(j - 1)
-            logits(j - 1)
-            on_vector = 5 if j == 1 else (1 if j < LAG - 1 else 0)
-            for piece in range(3, XI_PIECES - on_vector):
-                group_x(j - 1, piece)
-            when(j, turn_y, 0)
-            when(j, turn_y, 1)
+                quantize_y(0)
+            when(q - 1, mean_square)
+            when(q - 1, inverse_root_pow)
+            if j > 1:
+                logits(j - 1)
+            turn_y(j, 0)
+            turn_y(j, 1)
+            if j == 1:
+                logits(0)
+            open_x(j)
+            if j > 1:
+                group_x(j, share(j), D)
+            when(j - 3, row_factor)
+            scale_y(j, 1)
+            empty_y(j, 0)
+            empty_y(j, 1)
+            turn_y(j, 2)
+            turn_y(j, 3)
             add_bias(j - 1, 0)
             add_bias(j - 1, 1)
+            empty_y(j, 2)
+            empty_y(j, 3)
+            if j == 1:
+                group_x_half(j, 0)
+                group_x_half(j, 1)
+                group_x_vector(0)
+            group_x_vector(j)
+            when(j - 3, reweight)
+            quantize_x(j - 1)
+            when(q, pool_matmul, "s", both)
+            when(j - 3, mass_matmul, "logit")
             when(j - 2, row_max, 0)
             when(j - 2, row_max, 1)
-            when(j, group_x, 0)
             when(j - 2, exponentiate, 0)
             when(j - 2, exponentiate, 1)
-            when(j, scale_y, 2)
-            when(j, scale_y, 3)
-            for piece in range(XI_PIECES - on_vector, XI_PIECES):
-                group_x(j - 1, piece, nc.vector.tensor_copy)
-            when(j, empty_y, 0)
-            when(j, empty_y, 1)
             turn_logits(j - 1)
-            when(j, turn_y, 2)
-            when(j, turn_y, 3)
-            when(j, group_x, 1)
+            when(q - 2, normalise, 1, False)
             when(q, centre, 0)
             when(q, centre, 1)
-            when(q, mean_square)
-            when(q, inverse_root_pow)
-            when(j, empty_y, 2)
-            when(j, empty_y, 3)
-            when(j, group_x, 2)
-            when(q + 1, pool_matmul, "s", both)
-            when(j - 2, invert_sums)
-            when(j - 2, mass_matmul)
-            quantize_x(j - 1)
-            when(j - 2, row_factor)
-            when(q - 1, normalise, 1, j == UNITS)
-            when(j - 2, reweight)
+            when(j - 3, quantize_r)
             when(j + AHEAD - 1, load_unit)
 
-        last = UNITS - 1
-        q = UNITS + 1 - LAG
-        assert q == UNITS - 4
-        row_max(last, 0)
-        row_max(last, 1)
-        mass_collect(last - 1)
-        quantize_r(last - 1)
-        exponentiate(last, 0)
-        exponentiate(last, 1)
-        pool_matmul(q + 1, "turn", both)
-        centre(q, 0)
-        centre(q, 1)
-        pool_matmul(UNITS - 2, "s", [0])
-        mean_square(q)
-        centre(q + 1, 0)
-        invert_sums(last)
-        mass_matmul(last)
-        centre(q + 1, 1)
-        row_factor(last)
-        normalise(q - 1)
-        pool_matmul(UNITS - 1, "turn", [0])
-        root(q)
-        mean_square(q + 1)
-        root(q + 1)
-        reweight(last)
-        mass_collect(last)
-        quantize_r(last)
-        pool_matmul(UNITS - 2, "s", [1])
-        pool_matmul(UNITS - 1, "turn", [1])
-        invert_root(q)
-        centre(UNITS - 2, 0)
-        centre(UNITS - 2, 1)
-        mean_square(UNITS - 2)
-        centre(UNITS - 1, 0)
-        centre(UNITS - 1, 1)
-        invert_root(q + 1)
-        normalise(q)
-        normalise(q + 1)
-        root(UNITS - 2)
-        mean_square(UNITS - 1)
-        invert_root(UNITS - 2)
-        root(UNITS - 1)
-        normalise(UNITS - 2)
-        invert_root(UNITS - 1)
-        normalise(UNITS - 1, 2)
+        quantize_y(7)
+        mass_collect(4)
+        logits(7)
+        pool_matmul(3, "s", both)
+        mean_square(2)
+        inverse_root_pow(2)
+        row_max(6, 0)
+        row_max(6, 1)
+        exponentiate(6, 0)
+        exponentiate(6, 1)
+        add_bias(7, 0)
+        add_bias(7, 1)
+        invert_sums(5)
+        turn_logits(7)
+        mass_matmul(5, "logit")
+        quantize_x(7)
+        row_factor(5)
+        centre(3, 0)
+        centre(3, 1)
+        normalise(1, 1, True)
+        mean_square(3)
+        normalise(2, 1, True)
+        reweight(5)
+        invert_sums(6)
+        quantize_r(5)
+        mass_collect(5)
+        row_max(7, 0)
+        row_factor(6)
+        row_max(7, 1)
+        exponentiate(7, 0)
+        exponentiate(7, 1)
+        root(3)
+        pool_matmul(4, "s", both)
+        pool_matmul(5, "turn", both)
+        mass_matmul(6, "logit")
+        reweight(6)
+        centre(4, 0)
+        quantize_r(6)
+        invert_sums(7)
+        centre(4, 1)
+        mean_square(4)
+        row_factor(7)
+        mass_collect(6)
+        invert_root(3)
+        normalise(3, 1, True)
+        root(4)
+        pool_matmul(6, "zb", [0])
+        pool_matmul(7, "s", [0])
+        mass_matmul(7, "logit")
+        reweight(7)
+        centre(5, 0)
+        quantize_r(7)
+        pool_matmul(6, "zb", [1])
+        pool_matmul(7, "s", [1])
+        centre(5, 1)
+        invert_root(4)
+        mass_collect(7)
+        mean_square(5)
+        root(5)
+        centre(6, 0)
+        centre(6, 1)
+        mean_square(6)
+        centre(7, 0)
+        centre(7, 1)
+        root(6)
+        mean_square(7)
+        root(7)
+        normalise(4)
+        invert_root(5)
+        invert_root(6)
+        normalise(5)
+        normalise(6)
+        invert_root(7)
+        normalise(7, 2)

@@ -25,7 +25,7 @@ E_PASSES = E // PASS
 N_PASSES = N // PASS
 HALVES = K // P
 UNITS = B * N_PASSES
-SHARES = [0, 512, 512, 128, 0, 0, 0, 0]
+EXTRA_COLS = [256, 256, 256, 0, 0, 0, 0, 0]
 LAG = 5
 AHEAD = 4
 MASS_COLS = 64
@@ -48,7 +48,7 @@ def tile_crossmodalreweightedvlad_kernel(tc, y_bytes, y_scale, w, b, t, x, c, ou
         nc.vector.memset(warm_in[:], 0.0)
         nc.scalar.activation(out=warm_out[:], in_=warm_in[:], func=ACT.Exp)
 
-        scale_rows = const.tile([P, 2 * E], F32, name="scale_rows")
+        scale_cols = const.tile([P, E_PASSES, PACK], F32, name="scale_cols")
         w_raw = const.tile([P, E_PASSES, PACK, K], BF16, name="w_raw")
         w_grouped = const.tile([P, E_PASSES, K, PACK], BF16, name="w_grouped", align_bytes=64)
         w_codes = const.tile([P, E_PASSES, K], U32, name="w_codes", align_bytes=64)
@@ -58,7 +58,7 @@ def tile_crossmodalreweightedvlad_kernel(tc, y_bytes, y_scale, w, b, t, x, c, ou
         t_cols = const.tile([P, N_PASSES, PACK], BF16, name="t_cols")
         c_rows = const.tile([P, HALVES, D], BF16, name="c_rows")
 
-        y_raw, x_raw, y_scaled, y_turned, y_grouped, y_q = {}, {}, {}, {}, {}, {}
+        y_raw, x_raw, y_wide, y_turned, y_grouped, y_q = {}, {}, {}, {}, {}, {}
         lt, zt, zb, neg_max, expd, sums, recip, factor = {}, {}, {}, {}, {}, {}, {}, {}
         r_grouped, r_q, x_grouped, x_q, mass, s_bank, neg_v, mean_sq, rstd = {}, {}, {}, {}, {}, {}, {}, {}, {}
 
@@ -85,27 +85,30 @@ def tile_crossmodalreweightedvlad_kernel(tc, y_bytes, y_scale, w, b, t, x, c, ou
             nc.vector.quantize_mx(out=codes[:].bitcast(FP8X4), scales=scales[:], in_=src)
             return codes, scales
 
-        def scale_y(u, half):
-            y_scaled[u, half] = work.tile([P, 2 * E], BF16, name="y_scaled", bufs=3)
-            nc.vector.tensor_tensor(out=y_scaled[u, half][:], in0=y_raw[u, half].bitcast(FP8),
-                                    in1=scale_rows[:], op=ALU.mult)
+        def widen_y(u, half):
+            y_wide[u, half] = work.tile([P, 2 * E], BF16, name="y_wide", bufs=3)
+            nc.scalar.copy(out=y_wide[u, half][:], in_=y_raw[u, half].bitcast(FP8))
 
         def turn_y(u, s):
-            words = y_scaled[u, s // 2][:].bitcast(F32)[:, (s % 2) * E // 2:(s % 2 + 1) * E // 2]
-            y_turned[u, s] = psum.tile([P, E_PASSES, 2, P], F32, name="y_turned", tag="turn")
+            words = y_wide[u, s // 2][:].bitcast(F32)[:, (s % 2) * E // 2:(s % 2 + 1) * E // 2]
+            y_turned[u, s] = psum.tile([P, 2, E_PASSES, P], F32, name="y_turned", tag="turn")
             for g in range(E_PASSES):
                 for pair in range(2):
-                    nc.tensor.transpose(y_turned[u, s][:, g, pair, :],
+                    nc.tensor.transpose(y_turned[u, s][:, pair, g, :],
                                         words[:, 2 * P * g + pair:2 * P * (g + 1):2], ident[:])
 
-        def empty_y(u, s):
+        def scale_y(u, s):
             if s == 0:
-                y_grouped[u] = work.tile([P, E_PASSES, PACK, 2 * P], F32, name="y_grouped", align_bytes=64)
-            nc.scalar.copy(out=y_grouped[u][:, :, s, :].rearrange("p g (n u) -> p g n u", u=2),
-                           in_=y_turned[u, s][:].rearrange("p g u n -> p g n u"))
+                y_grouped[u] = work.tile([P, E_PASSES, PACK, PASS], BF16, name="y_grouped", align_bytes=64)
+            turned = y_turned[u, s][:].rearrange("p u g n -> p (u g n)").bitcast(BF16)
+            nc.vector.tensor_tensor(
+                out=y_grouped[u][:, :, s, :].rearrange("p g (n u e) -> p g n u e", u=2, e=2),
+                in0=turned.rearrange("p (u g n e) -> p g n u e", u=2, g=E_PASSES, e=2),
+                in1=scale_cols[:].rearrange("p g (u e) -> p g u e", u=2).unsqueeze(2).to_broadcast([P, E_PASSES, P, 2, 2]),
+                op=ALU.mult)
 
         def quantize_y(u):
-            y_q[u] = quantize("y", y_grouped[u][:].rearrange("p g s n -> p (g s n)").bitcast(BF16), E_PASSES * PASS, 2)
+            y_q[u] = quantize("y", y_grouped[u][:].rearrange("p g s n -> p (g s n)"), E_PASSES * PASS, 2)
 
         def logits(u):
             codes, scales = y_q[u]
@@ -137,7 +140,7 @@ def tile_crossmodalreweightedvlad_kernel(tc, y_bytes, y_scale, w, b, t, x, c, ou
 
         def exponentiate(u, half):
             if half == 0:
-                expd[u] = work.tile([P, PACK, K], F32, name="expd")
+                expd[u] = work.tile([P, PACK, K], F32, name="expd", bufs=3)
                 sums[u] = work.tile([P, PACK], F32, name="sums")
             for s2 in range(2):
                 s = 2 * half + s2
@@ -145,46 +148,50 @@ def tile_crossmodalreweightedvlad_kernel(tc, y_bytes, y_scale, w, b, t, x, c, ou
                                      bias=neg_max[u, half][:, s2:s2 + 1], scale=-1.0, accum_out=sums[u][:, s:s + 1])
 
         def invert_sums(u):
-            recip[u] = work.tile([P, PACK], F32, name="recip")
+            recip[u] = work.tile([P, PACK], F32, name="recip", bufs=3)
             nc.vector.reciprocal(out=recip[u][:], in_=sums[u][:])
 
         def row_factor(u):
             factor[u] = work.tile([P, PACK], F32, name="factor")
             nc.vector.tensor_tensor(out=factor[u][:], in0=recip[u][:], in1=t_cols[:, u % N_PASSES, :], op=ALU.mult)
 
-        def reweight(u):
+        def reweight(u, engine):
             r_grouped[u] = work.tile([P, K, PACK], BF16, name="r_grouped", align_bytes=64)
-            nc.vector.tensor_tensor(out=r_grouped[u][:].rearrange("p (c i) s -> p c s i", i=2),
+            engine.tensor_tensor(out=r_grouped[u][:].rearrange("p (c i) s -> p c s i", i=2),
                                     in0=expd[u][:].rearrange("p s (c i) -> p c s i", i=2),
                                     in1=factor[u][:].unsqueeze(1).unsqueeze(3).to_broadcast([P, K // 2, PACK, 2]), op=ALU.mult)
+
+        def reweight_pool(u):
+            r_grouped[u] = work.tile([P, K, PACK], BF16, name="r_grouped", align_bytes=64)
+            nc.gpsimd.tensor_tensor(out=r_grouped[u][:], in0=expd[u][:].rearrange("p s k -> p k s"),
+                                    in1=factor[u][:].unsqueeze(1).to_broadcast([P, K, PACK]), op=ALU.mult)
 
         def quantize_r(u):
             r_q[u] = quantize("r", r_grouped[u][:].rearrange("p k s -> p (k s)"), K, LAG)
 
-        def share(u):
-            return SHARES[u]
+        def x_views(u, dh, lo, hi):
+            return (x_grouped[u, dh][:, lo:hi, :].rearrange("p (c i) s -> p c s i", i=4),
+                    x_raw[u][:, :, dh * BANK + lo:dh * BANK + hi].rearrange("p s (c i) -> p c s i", i=4))
 
-        def group_x_half(u, half, copy=nc.scalar.copy):
-            mid = (share(u) + D) // 2
-            group_x(u, *((share(u), mid), (mid, D))[half], copy)
+        def pool_copy(u, dh, cols):
+            nc.gpsimd.tensor_scalar(out=x_grouped[u, dh][:, :cols, :],
+                                    in0=x_raw[u][:, :, dh * BANK:dh * BANK + cols].rearrange("p s d -> p d s"),
+                                    scalar1=1.0, scalar2=0.0, op0=ALU.mult, op1=ALU.add)
 
-        def open_x(u):
-            x_grouped[u] = work.tile([P, D, PACK], BF16, name="x_grouped", align_bytes=64)
+        def group_x_pool(u):
+            x_grouped[u, 0] = work.tile([P, BANK, PACK], BF16, name="x_grouped", tag="x_pool", bufs=1, align_bytes=64)
+            pool_copy(u, 0, BANK)
+            if EXTRA_COLS[u]:
+                pool_copy(u, 1, EXTRA_COLS[u])
 
-        def x_views(u, lo, hi):
-            return (x_grouped[u][:, lo:hi, :].rearrange("p (c i) s -> p c s i", i=4),
-                    x_raw[u][:, :, lo:hi].rearrange("p s (c i) -> p c s i", i=4))
-
-        def group_x(u, lo, hi, copy=nc.scalar.copy):
-            dst, src = x_views(u, lo, hi)
-            copy(out=dst, in_=src)
-
-        def group_x_vector(u):
-            if share(u):
-                group_x(u, 0, share(u), nc.vector.tensor_copy)
+        def group_x_scalar(u):
+            x_grouped[u, 1] = work.tile([P, BANK, PACK], BF16, name="x_grouped", tag="x_scalar", align_bytes=64)
+            dst, src = x_views(u, 1, EXTRA_COLS[u], BANK)
+            nc.scalar.copy(out=dst, in_=src)
 
         def quantize_x(u):
-            x_q[u] = quantize("x", x_grouped[u][:].rearrange("p d s -> p (d s)"), D, LAG + 1)
+            for dh in (1, 0):
+                x_q[u, dh] = quantize("x", x_grouped[u, dh][:].rearrange("p d s -> p (d s)"), BANK, 2 * (LAG + 1))
 
         def mass_matmul(u, tag):
             mass_bank[u] = psum.tile([P, HALVES, MASS_COLS], F32, name="mass_bank", tag=tag)
@@ -207,13 +214,12 @@ def tile_crossmodalreweightedvlad_kernel(tc, y_bytes, y_scale, w, b, t, x, c, ou
             for dh in range(D // BANK):
                 if passes[0] == 0:
                     s_bank[q, dh] = psum.tile([P, BANK], F32, name="s_bank", tag=tag)
-                feats = slice(dh * BANK, (dh + 1) * BANK)
                 for g in passes:
                     r_codes, r_scales = r_q[N_PASSES * i + g]
-                    x_codes, x_scales = x_q[N_PASSES * i + g]
+                    x_codes, x_scales = x_q[N_PASSES * i + g, dh]
                     nc.tensor.matmul_mx(out=s_bank[q, dh][:], lhsT=r_codes[:, cols].bitcast(FP8X4),
-                                        lhsT_scale=r_scales[:, cols], rhs=x_codes[:, feats].bitcast(FP8X4),
-                                        rhs_scale=x_scales[:, feats], start=(g == 0), stop=(g == N_PASSES - 1))
+                                        lhsT_scale=r_scales[:, cols], rhs=x_codes[:].bitcast(FP8X4),
+                                        rhs_scale=x_scales[:], start=(g == 0), stop=(g == N_PASSES - 1))
 
         def centre(q, dh):
             i, h = divmod(q, HALVES)
@@ -243,12 +249,15 @@ def tile_crossmodalreweightedvlad_kernel(tc, y_bytes, y_scale, w, b, t, x, c, ou
             rstd[q] = work.tile([P, 1], F32, name="rstd_tail", bufs=4)
             nc.vector.reciprocal(out=rstd[q][:], in_=rms[q][:])
 
-        def normalise(q, parts=1, on_scalar=False):
+        def normalise(q, parts=1, on_scalar=False, on_pool=False):
             i, h = divmod(q, HALVES)
             for part in range(parts):
                 feats = slice(part * D // parts, (part + 1) * D // parts)
                 result = work.tile([P, D // parts], F32, name="result", bufs=5)
-                if on_scalar:
+                if on_pool:
+                    nc.gpsimd.tensor_scalar(out=result[:], in0=neg_v[q][:, feats], scalar1=rstd[q][:], scalar2=0.0,
+                                            op0=ALU.mult, op1=ALU.add)
+                elif on_scalar:
                     nc.scalar.activation(out=result[:], in_=neg_v[q][:, feats], func=ACT.Copy, scale=rstd[q][:])
                 else:
                     nc.vector.tensor_scalar(out=result[:], in0=neg_v[q][:, feats], scalar1=rstd[q][:], scalar2=None,
@@ -258,27 +267,17 @@ def tile_crossmodalreweightedvlad_kernel(tc, y_bytes, y_scale, w, b, t, x, c, ou
         rms, mass_bank = {}, {}
         both = list(range(N_PASSES))
 
-        per_part = E // P
-        scale_cols = const.tile([P, per_part], F32, name="scale_cols")
-        nc.sync.dma_start(out=scale_cols[:], in_=y_scale.rearrange("a o (p j) -> p (a o j)", p=P))
-        nc.sync.dma_start(out=w_raw[:], in_=w.rearrange("(g p t) k -> p g t k", p=P, t=PACK))
         load_y(0, [0])
-        load_x(0)
+        nc.sync.dma_start(out=w_raw[:], in_=w.rearrange("(g p t) k -> p g t k", p=P, t=PACK))
+        nc.sync.dma_start(out=scale_cols[:], in_=y_scale.rearrange("a o (g p t) -> p (a o g) t", p=P, t=PACK))
         load_y(0, [1])
+        load_x(0)
         nc.sync.dma_start(out=b_cols[:], in_=b.rearrange("(p h) -> p h", h=HALVES))
         nc.sync.dma_start(out=t_cols[:], in_=t.rearrange("(g p s) -> p g s", p=P, s=PACK))
         load_unit(1)
         nc.sync.dma_start(out=c_rows[:], in_=c.rearrange("(p h) d -> p h d", h=HALVES))
         for u in range(2, AHEAD):
             load_unit(u)
-        for half in range(2):
-            spread = psum.tile([P, PACK, P], F32, name="spread", tag="zb")
-            for jj in range(PACK):
-                col = half * PACK + jj
-                nc.tensor.transpose(spread[:, jj, :], scale_cols[:, col:col + 1].to_broadcast([P, P]), ident[:])
-            nc.scalar.copy(out=scale_rows[:, :E].rearrange("q (p j) -> q p j", j=per_part)[:, :, half * PACK:(half + 1) * PACK],
-                           in_=spread[:].rearrange("q j p -> q p j"))
-        nc.scalar.copy(out=scale_rows[:, E:], in_=scale_rows[:, :E])
         for g in range(E_PASSES):
             nc.vector.tensor_copy(out=w_grouped[:, g, :, :].rearrange("p (h m) t -> p h m t", h=HALVES),
                                   in_=w_raw[:, g, :, :].rearrange("p t (m h) -> p h m t", h=HALVES))
@@ -292,74 +291,53 @@ def tile_crossmodalreweightedvlad_kernel(tc, y_bytes, y_scale, w, b, t, x, c, ou
             if 0 <= u < UNITS:
                 step(u, *args)
 
-        quantize_w()
-        scale_y(0, 0)
-        scale_y(0, 1)
-        nc.vector.tensor_scalar(out=neg_b[:], in0=b_cols[:], scalar1=-1.0, scalar2=None, op0=ALU.mult)
-        open_x(0)
-        group_x_half(0, 0)
+        widen_y(0, 0)
         turn_y(0, 0)
         turn_y(0, 1)
-        empty_y(0, 0)
-        empty_y(0, 1)
-        turn_y(0, 2)
-        turn_y(0, 3)
-        empty_y(0, 2)
-        empty_y(0, 3)
-        group_x_half(0, 1)
+        quantize_w()
+        nc.vector.tensor_scalar(out=neg_b[:], in0=b_cols[:], scalar1=-1.0, scalar2=None, op0=ALU.mult)
 
-        for j in range(1, UNITS):
+        for j in range(UNITS):
             q = j - LAG
-            if j > 1:
-                quantize_y(j - 1)
-            when(j - 4, mass_collect)
-            when(j - 3, invert_sums)
-            scale_y(j, 0)
-            if j == 1:
-                quantize_y(0)
+            widen_y(j, 1)
+            group_x_scalar(j)
+            when(j - 1, quantize_y)
+            when(j - 3, row_factor)
+            when(j - 1, logits)
+            when(j - 4, quantize_r)
+            when(q - 2, normalise, 1, False)
+            when(j - 1, quantize_x)
+            when(q, pool_matmul, "s", both)
+            group_x_pool(j)
+            when(j - 3, reweight_pool)
             when(q - 1, mean_square)
             when(q - 1, inverse_root_pow)
-            if j > 1:
-                logits(j - 1)
-            turn_y(j, 0)
-            turn_y(j, 1)
-            if j == 1:
-                logits(0)
-            open_x(j)
-            if j > 1:
-                group_x(j, share(j), D)
-            when(j - 3, row_factor)
-            scale_y(j, 1)
-            empty_y(j, 0)
-            empty_y(j, 1)
+            when(j - 1, add_bias, 0)
+            when(j - 1, add_bias, 1)
+            scale_y(j, 0)
             turn_y(j, 2)
+            scale_y(j, 1)
             turn_y(j, 3)
-            add_bias(j - 1, 0)
-            add_bias(j - 1, 1)
-            empty_y(j, 2)
-            empty_y(j, 3)
-            if j == 1:
-                group_x_half(j, 0)
-                group_x_half(j, 1)
-                group_x_vector(0)
-            group_x_vector(j)
-            when(j - 3, reweight)
-            quantize_x(j - 1)
-            when(q, pool_matmul, "s", both)
             when(j - 3, mass_matmul, "logit")
             when(j - 2, row_max, 0)
             when(j - 2, row_max, 1)
             when(j - 2, exponentiate, 0)
             when(j - 2, exponentiate, 1)
-            turn_logits(j - 1)
-            when(q - 2, normalise, 1, False)
+            when(j - 1, turn_logits)
+            when(j + 1, widen_y, 0)
+            scale_y(j, 2)
+            scale_y(j, 3)
+            when(j + 1, turn_y, 0)
+            when(j + 1, turn_y, 1)
             when(q, centre, 0)
             when(q, centre, 1)
-            when(j - 3, quantize_r)
-            when(j + AHEAD - 1, load_unit)
+            when(j - 3, mass_collect)
+            when(j - 2, invert_sums)
+            if j >= 1:
+                when(j + AHEAD - 1, load_unit)
 
         quantize_y(7)
-        mass_collect(4)
+        row_factor(5)
         logits(7)
         pool_matmul(3, "s", both)
         mean_square(2)
@@ -370,30 +348,29 @@ def tile_crossmodalreweightedvlad_kernel(tc, y_bytes, y_scale, w, b, t, x, c, ou
         exponentiate(6, 1)
         add_bias(7, 0)
         add_bias(7, 1)
-        invert_sums(5)
         turn_logits(7)
         mass_matmul(5, "logit")
+        quantize_r(4)
         quantize_x(7)
-        row_factor(5)
+        reweight(5, nc.vector)
         centre(3, 0)
         centre(3, 1)
         normalise(1, 1, True)
         mean_square(3)
         normalise(2, 1, True)
-        reweight(5)
-        invert_sums(6)
         quantize_r(5)
-        mass_collect(5)
+        invert_sums(6)
         row_max(7, 0)
         row_factor(6)
         row_max(7, 1)
+        mass_collect(5)
         exponentiate(7, 0)
         exponentiate(7, 1)
         root(3)
         pool_matmul(4, "s", both)
         pool_matmul(5, "turn", both)
         mass_matmul(6, "logit")
-        reweight(6)
+        reweight(6, nc.vector)
         centre(4, 0)
         quantize_r(6)
         invert_sums(7)
@@ -401,34 +378,34 @@ def tile_crossmodalreweightedvlad_kernel(tc, y_bytes, y_scale, w, b, t, x, c, ou
         mean_square(4)
         row_factor(7)
         mass_collect(6)
-        invert_root(3)
-        normalise(3, 1, True)
         root(4)
         pool_matmul(6, "zb", [0])
         pool_matmul(7, "s", [0])
         mass_matmul(7, "logit")
-        reweight(7)
+        reweight(7, nc.vector)
+        invert_root(3)
+        normalise(3, 1, True)
         centre(5, 0)
         quantize_r(7)
         pool_matmul(6, "zb", [1])
         pool_matmul(7, "s", [1])
-        centre(5, 1)
-        invert_root(4)
         mass_collect(7)
+        invert_root(4)
+        centre(5, 1)
+        normalise(4, 1, False, True)
         mean_square(5)
-        root(5)
         centre(6, 0)
         centre(6, 1)
+        root(5)
         mean_square(6)
         centre(7, 0)
         centre(7, 1)
         root(6)
         mean_square(7)
         root(7)
-        normalise(4)
         invert_root(5)
-        invert_root(6)
         normalise(5)
+        invert_root(6)
         normalise(6)
         invert_root(7)
         normalise(7, 2)

@@ -25,10 +25,20 @@ E_PASSES = E // PASS
 N_PASSES = N // PASS
 HALVES = K // P
 UNITS = B * N_PASSES
-EXTRA_COLS = [256, 256, 256, 0, 0, 0, 0, 0]
-LAG = 5
+ALL_PASSES = list(range(N_PASSES))
+
+REWEIGHT_LAG = 3
+POOL_LAG = 5
 AHEAD = 4
 MASS_COLS = 64
+WIDE_EXTRA = 256
+NARROW_EXTRA = 128
+
+
+def pool_extra(u):
+    if u == 0 or u >= POOL_LAG:
+        return NARROW_EXTRA
+    return WIDE_EXTRA if u < REWEIGHT_LAG else 0
 
 
 def tile_crossmodalreweightedvlad_kernel(tc, y_bytes, y_scale, w, b, t, x, c, out):
@@ -59,21 +69,22 @@ def tile_crossmodalreweightedvlad_kernel(tc, y_bytes, y_scale, w, b, t, x, c, ou
         c_rows = const.tile([P, HALVES, D], BF16, name="c_rows")
 
         y_raw, x_raw, y_wide, y_turned, y_grouped, y_q = {}, {}, {}, {}, {}, {}
-        lt, zt, zb, neg_max, expd, sums, recip, factor = {}, {}, {}, {}, {}, {}, {}, {}
-        r_grouped, r_q, x_grouped, x_q, mass, s_bank, neg_v, mean_sq, rstd = {}, {}, {}, {}, {}, {}, {}, {}, {}
+        logit_bank, neg_z, neg_z_turned, neg_max, expd, sums, recip, factor = {}, {}, {}, {}, {}, {}, {}, {}
+        r_grouped, r_q, x_grouped, x_q, mass_bank, neg_mass = {}, {}, {}, {}, {}, {}
+        s_bank, v, mean_sq, rms, rstd = {}, {}, {}, {}, {}
 
-        def load_y(u, halves):
+        def load_y(u, pairs):
             i, g = divmod(u, N_PASSES)
-            rows = work.tile([P, len(halves) * 2 * E], U8, name="y_raw", bufs=AHEAD + 2)
+            rows = work.tile([P, len(pairs) * 2 * E], U8, name="y_raw", bufs=AHEAD + 2)
             src = y_bytes[i, g * PASS:(g + 1) * PASS, :].rearrange("(p s) e -> p (s e)", s=PACK)
-            nc.sync.dma_start(out=rows[:], in_=src[:, halves[0] * 2 * E:(halves[-1] + 1) * 2 * E])
-            for n, half in enumerate(halves):
-                y_raw[u, half] = rows[:, n * 2 * E:(n + 1) * 2 * E]
+            nc.sync.dma_start(out=rows[:], in_=src[:, pairs[0] * 2 * E:(pairs[-1] + 1) * 2 * E])
+            for n, pair in enumerate(pairs):
+                y_raw[u, pair] = rows[:, n * 2 * E:(n + 1) * 2 * E]
 
         def load_x(u):
             i, g = divmod(u, N_PASSES)
             x_raw[u] = work.tile([P, PACK, D], BF16, name="x_raw", bufs=AHEAD)
-            nc.sync.dma_start(out=x_raw[u][:], in_=x[i, g * PASS:(g + 1) * PASS, :].rearrange("(p t) d -> p t d", t=PACK))
+            nc.sync.dma_start(out=x_raw[u][:], in_=x[i, g * PASS:(g + 1) * PASS, :].rearrange("(p s) d -> p s d", s=PACK))
 
         def load_unit(u):
             load_y(u, [0, 1])
@@ -85,26 +96,33 @@ def tile_crossmodalreweightedvlad_kernel(tc, y_bytes, y_scale, w, b, t, x, c, ou
             nc.vector.quantize_mx(out=codes[:].bitcast(FP8X4), scales=scales[:], in_=src)
             return codes, scales
 
-        def widen_y(u, half):
-            y_wide[u, half] = work.tile([P, 2 * E], BF16, name="y_wide", bufs=3)
-            nc.scalar.copy(out=y_wide[u, half][:], in_=y_raw[u, half].bitcast(FP8))
+        def quantize_w():
+            nc.vector.quantize_mx(out=w_codes[:].rearrange("p g k -> p (g k)").bitcast(FP8X4),
+                                  scales=w_scales[:].rearrange("p g k -> p (g k)"),
+                                  in_=w_grouped[:].rearrange("p g k s -> p (g k s)"))
+
+        def widen_y(u, slots, copy=nc.scalar.copy):
+            wide = work.tile([P, len(slots) * E], BF16, name="y_wide", bufs=5)
+            first = slots[0] % 2 * E
+            copy(out=wide[:], in_=y_raw[u, slots[0] // 2][:, first:first + len(slots) * E].bitcast(FP8))
+            for n, s in enumerate(slots):
+                y_wide[u, s] = wide[:].bitcast(F32)[:, n * E // 2:(n + 1) * E // 2]
 
         def turn_y(u, s):
-            words = y_wide[u, s // 2][:].bitcast(F32)[:, (s % 2) * E // 2:(s % 2 + 1) * E // 2]
             y_turned[u, s] = psum.tile([P, 2, E_PASSES, P], F32, name="y_turned", tag="turn")
             for g in range(E_PASSES):
-                for pair in range(2):
-                    nc.tensor.transpose(y_turned[u, s][:, pair, g, :],
-                                        words[:, 2 * P * g + pair:2 * P * (g + 1):2], ident[:])
+                for word in range(2):
+                    nc.tensor.transpose(y_turned[u, s][:, word, g, :],
+                                        y_wide[u, s][:, 2 * P * g + word:2 * P * (g + 1):2], ident[:])
 
         def scale_y(u, s):
             if s == 0:
                 y_grouped[u] = work.tile([P, E_PASSES, PACK, PASS], BF16, name="y_grouped", align_bytes=64)
-            turned = y_turned[u, s][:].rearrange("p u g n -> p (u g n)").bitcast(BF16)
+            turned = y_turned[u, s][:].rearrange("p a g n -> p (a g n)").bitcast(BF16)
             nc.vector.tensor_tensor(
-                out=y_grouped[u][:, :, s, :].rearrange("p g (n u e) -> p g n u e", u=2, e=2),
-                in0=turned.rearrange("p (u g n e) -> p g n u e", u=2, g=E_PASSES, e=2),
-                in1=scale_cols[:].rearrange("p g (u e) -> p g u e", u=2).unsqueeze(2).to_broadcast([P, E_PASSES, P, 2, 2]),
+                out=y_grouped[u][:, :, s, :].rearrange("p g (n a e) -> p g n a e", a=2, e=2),
+                in0=turned.rearrange("p (a g n e) -> p g n a e", a=2, g=E_PASSES, e=2),
+                in1=scale_cols[:].rearrange("p g (a e) -> p g a e", a=2).unsqueeze(2).to_broadcast([P, E_PASSES, P, 2, 2]),
                 op=ALU.mult)
 
         def quantize_y(u):
@@ -113,39 +131,41 @@ def tile_crossmodalreweightedvlad_kernel(tc, y_bytes, y_scale, w, b, t, x, c, ou
         def logits(u):
             codes, scales = y_q[u]
             for h in range(HALVES):
-                lt[u, h] = psum.tile([P, PASS], F32, name="lt", tag="logit")
+                logit_bank[u, h] = psum.tile([P, PASS], F32, name="logit_bank", tag="logit")
                 cols = slice(h * P, (h + 1) * P)
                 for g in range(E_PASSES):
                     toks = slice(g * PASS, (g + 1) * PASS)
-                    nc.tensor.matmul_mx(out=lt[u, h][:], lhsT=w_codes[:, g, cols].bitcast(FP8X4),
+                    nc.tensor.matmul_mx(out=logit_bank[u, h][:], lhsT=w_codes[:, g, cols].bitcast(FP8X4),
                                         lhsT_scale=w_scales[:, g, cols], rhs=codes[:, toks].bitcast(FP8X4),
                                         rhs_scale=scales[:, toks], start=(g == 0), stop=(g == E_PASSES - 1))
 
-        def add_bias(u, h):
-            zt[u, h] = work.tile([P, PASS], F32, name="zt", bufs=2)
-            nc.scalar.activation(out=zt[u, h][:], in_=lt[u, h][:], func=ACT.Identity,
-                                 bias=neg_b[:, h:h + 1], scale=-1.0)
+        def add_bias(u):
+            for h in range(HALVES):
+                neg_z[u, h] = work.tile([P, PASS], F32, name="neg_z", bufs=2)
+                nc.scalar.activation(out=neg_z[u, h][:], in_=logit_bank[u, h][:], func=ACT.Identity,
+                                     bias=neg_b[:, h:h + 1], scale=-1.0)
 
-        def turn_logits(u):
-            for half in range(2):
-                zb[u, half] = psum.tile([P, 2, K], F32, name="zb", tag="zb")
-                for s2 in range(2):
-                    s = 2 * half + s2
+        def turn_logits(u, tag):
+            for pair in range(2):
+                neg_z_turned[u, pair] = psum.tile([P, 2, K], F32, name="neg_z_turned", tag=tag)
+                for n in range(2):
+                    s = 2 * pair + n
                     for h in range(HALVES):
-                        nc.tensor.transpose(zb[u, half][:, s2, h * P:(h + 1) * P], zt[u, h][:, s * P:(s + 1) * P], ident[:])
+                        nc.tensor.transpose(neg_z_turned[u, pair][:, n, h * P:(h + 1) * P],
+                                            neg_z[u, h][:, s * P:(s + 1) * P], ident[:])
 
-        def row_max(u, half):
-            neg_max[u, half] = work.tile([P, 2], F32, name="neg_max", bufs=4)
-            nc.vector.tensor_reduce(out=neg_max[u, half][:], in_=zb[u, half][:], axis=AXIS.X, op=ALU.min)
+        def row_max(u):
+            for pair in range(2):
+                neg_max[u, pair] = work.tile([P, 2], F32, name="neg_max", bufs=4)
+                nc.vector.tensor_reduce(out=neg_max[u, pair][:], in_=neg_z_turned[u, pair][:], axis=AXIS.X, op=ALU.min)
 
-        def exponentiate(u, half):
-            if half == 0:
-                expd[u] = work.tile([P, PACK, K], F32, name="expd", bufs=3)
-                sums[u] = work.tile([P, PACK], F32, name="sums")
-            for s2 in range(2):
-                s = 2 * half + s2
-                nc.scalar.activation(out=expd[u][:, s, :], in_=zb[u, half][:, s2, :], func=ACT.Exp,
-                                     bias=neg_max[u, half][:, s2:s2 + 1], scale=-1.0, accum_out=sums[u][:, s:s + 1])
+        def exponentiate(u):
+            expd[u] = work.tile([P, PACK, K], F32, name="expd", bufs=3)
+            sums[u] = work.tile([P, PACK], F32, name="sums")
+            for s in range(PACK):
+                pair, n = divmod(s, 2)
+                nc.scalar.activation(out=expd[u][:, s, :], in_=neg_z_turned[u, pair][:, n, :], func=ACT.Exp,
+                                     bias=neg_max[u, pair][:, n:n + 1], scale=-1.0, accum_out=sums[u][:, s:s + 1])
 
         def invert_sums(u):
             recip[u] = work.tile([P, PACK], F32, name="recip", bufs=3)
@@ -155,11 +175,12 @@ def tile_crossmodalreweightedvlad_kernel(tc, y_bytes, y_scale, w, b, t, x, c, ou
             factor[u] = work.tile([P, PACK], F32, name="factor")
             nc.vector.tensor_tensor(out=factor[u][:], in0=recip[u][:], in1=t_cols[:, u % N_PASSES, :], op=ALU.mult)
 
-        def reweight(u, engine):
+        def reweight_vector(u):
             r_grouped[u] = work.tile([P, K, PACK], BF16, name="r_grouped", align_bytes=64)
-            engine.tensor_tensor(out=r_grouped[u][:].rearrange("p (c i) s -> p c s i", i=2),
-                                    in0=expd[u][:].rearrange("p s (c i) -> p c s i", i=2),
-                                    in1=factor[u][:].unsqueeze(1).unsqueeze(3).to_broadcast([P, K // 2, PACK, 2]), op=ALU.mult)
+            nc.vector.tensor_tensor(out=r_grouped[u][:].rearrange("p (k i) s -> p k s i", i=2),
+                                    in0=expd[u][:].rearrange("p s (k i) -> p k s i", i=2),
+                                    in1=factor[u][:].unsqueeze(1).unsqueeze(3).to_broadcast([P, K // 2, PACK, 2]),
+                                    op=ALU.mult)
 
         def reweight_pool(u):
             r_grouped[u] = work.tile([P, K, PACK], BF16, name="r_grouped", align_bytes=64)
@@ -167,11 +188,7 @@ def tile_crossmodalreweightedvlad_kernel(tc, y_bytes, y_scale, w, b, t, x, c, ou
                                     in1=factor[u][:].unsqueeze(1).to_broadcast([P, K, PACK]), op=ALU.mult)
 
         def quantize_r(u):
-            r_q[u] = quantize("r", r_grouped[u][:].rearrange("p k s -> p (k s)"), K, LAG)
-
-        def x_views(u, dh, lo, hi):
-            return (x_grouped[u, dh][:, lo:hi, :].rearrange("p (c i) s -> p c s i", i=4),
-                    x_raw[u][:, :, dh * BANK + lo:dh * BANK + hi].rearrange("p s (c i) -> p c s i", i=4))
+            r_q[u] = quantize("r", r_grouped[u][:].rearrange("p k s -> p (k s)"), K, POOL_LAG)
 
         def pool_copy(u, dh, cols):
             nc.gpsimd.tensor_scalar(out=x_grouped[u, dh][:, :cols, :],
@@ -181,20 +198,20 @@ def tile_crossmodalreweightedvlad_kernel(tc, y_bytes, y_scale, w, b, t, x, c, ou
         def group_x_pool(u):
             x_grouped[u, 0] = work.tile([P, BANK, PACK], BF16, name="x_grouped", tag="x_pool", bufs=1, align_bytes=64)
             pool_copy(u, 0, BANK)
-            if EXTRA_COLS[u]:
-                pool_copy(u, 1, EXTRA_COLS[u])
+            if pool_extra(u):
+                pool_copy(u, 1, pool_extra(u))
 
         def group_x_scalar(u):
             x_grouped[u, 1] = work.tile([P, BANK, PACK], BF16, name="x_grouped", tag="x_scalar", align_bytes=64)
-            dst, src = x_views(u, 1, EXTRA_COLS[u], BANK)
-            nc.scalar.copy(out=dst, in_=src)
+            nc.scalar.copy(out=x_grouped[u, 1][:, pool_extra(u):, :].rearrange("p (d i) s -> p d s i", i=4),
+                           in_=x_raw[u][:, :, BANK + pool_extra(u):].rearrange("p s (d i) -> p d s i", i=4))
 
         def quantize_x(u):
             for dh in (1, 0):
-                x_q[u, dh] = quantize("x", x_grouped[u, dh][:].rearrange("p d s -> p (d s)"), BANK, 2 * (LAG + 1))
+                x_q[u, dh] = quantize("x", x_grouped[u, dh][:].rearrange("p d s -> p (d s)"), BANK, 2 * (POOL_LAG + 1))
 
-        def mass_matmul(u, tag):
-            mass_bank[u] = psum.tile([P, HALVES, MASS_COLS], F32, name="mass_bank", tag=tag)
+        def mass_matmul(u):
+            mass_bank[u] = psum.tile([P, HALVES, MASS_COLS], F32, name="mass_bank", tag="logit")
             for h in range(HALVES):
                 for s in range(PACK):
                     nc.tensor.matmul(mass_bank[u][:, h, :], lhsT=expd[u][:, s, h * P:(h + 1) * P],
@@ -202,11 +219,13 @@ def tile_crossmodalreweightedvlad_kernel(tc, y_bytes, y_scale, w, b, t, x, c, ou
                                      start=(s == 0), stop=(s == PACK - 1))
 
         def mass_collect(u):
-            mass[u] = work.tile([P, HALVES], F32, name="mass", bufs=UNITS)
+            neg_mass[u] = work.tile([P, HALVES], F32, name="neg_mass", bufs=UNITS)
             if u % N_PASSES == 0:
-                nc.vector.tensor_scalar(out=mass[u][:], in0=mass_bank[u][:, :, 0], scalar1=-1.0, scalar2=None, op0=ALU.mult)
+                nc.vector.tensor_scalar(out=neg_mass[u][:], in0=mass_bank[u][:, :, 0], scalar1=-1.0, scalar2=None,
+                                        op0=ALU.mult)
             else:
-                nc.vector.tensor_tensor(out=mass[u][:], in0=mass[u - 1][:], in1=mass_bank[u][:, :, 0], op=ALU.subtract)
+                nc.vector.tensor_tensor(out=neg_mass[u][:], in0=neg_mass[u - 1][:], in1=mass_bank[u][:, :, 0],
+                                        op=ALU.subtract)
 
         def pool_matmul(q, tag, passes):
             i, h = divmod(q, HALVES)
@@ -224,16 +243,16 @@ def tile_crossmodalreweightedvlad_kernel(tc, y_bytes, y_scale, w, b, t, x, c, ou
         def centre(q, dh):
             i, h = divmod(q, HALVES)
             if dh == 0:
-                neg_v[q] = work.tile([P, D], F32, name="neg_v", bufs=5)
+                v[q] = work.tile([P, D], F32, name="v", bufs=5)
             feats = slice(dh * BANK, (dh + 1) * BANK)
-            nc.vector.scalar_tensor_tensor(out=neg_v[q][:, feats], in0=c_rows[:, h, feats], scalar=mass[N_PASSES * i + N_PASSES - 1][:, h:h + 1],
+            nc.vector.scalar_tensor_tensor(out=v[q][:, feats], in0=c_rows[:, h, feats],
+                                           scalar=neg_mass[N_PASSES * (i + 1) - 1][:, h:h + 1],
                                            in1=s_bank[q, dh][:], op0=ALU.mult, op1=ALU.add)
 
         def mean_square(q):
             squares = work.tile([P, D], BF16, name="squares", bufs=2)
             mean_sq[q] = work.tile([P, 1], F32, name="mean_sq", bufs=4)
-            nc.scalar.activation(out=squares[:], in_=neg_v[q][:], func=ACT.Square, scale=D ** -0.5,
-                                 accum_out=mean_sq[q][:])
+            nc.scalar.activation(out=squares[:], in_=v[q][:], func=ACT.Square, scale=D ** -0.5, accum_out=mean_sq[q][:])
 
         def inverse_root_pow(q):
             shifted = work.tile([P, 1], F32, name="shifted")
@@ -249,163 +268,160 @@ def tile_crossmodalreweightedvlad_kernel(tc, y_bytes, y_scale, w, b, t, x, c, ou
             rstd[q] = work.tile([P, 1], F32, name="rstd_tail", bufs=4)
             nc.vector.reciprocal(out=rstd[q][:], in_=rms[q][:])
 
-        def normalise(q, parts=1, on_scalar=False, on_pool=False):
+        def times_rstd_scalar(dst, src, q):
+            nc.scalar.activation(out=dst, in_=src, func=ACT.Copy, scale=rstd[q][:])
+
+        def times_rstd_pool(dst, src, q):
+            nc.gpsimd.tensor_scalar(out=dst, in0=src, scalar1=rstd[q][:], scalar2=0.0, op0=ALU.mult, op1=ALU.add)
+
+        def times_rstd_vector(dst, src, q):
+            nc.vector.tensor_scalar(out=dst, in0=src, scalar1=rstd[q][:], scalar2=None, op0=ALU.mult)
+
+        def normalise(q, times_rstd, parts=1):
             i, h = divmod(q, HALVES)
             for part in range(parts):
                 feats = slice(part * D // parts, (part + 1) * D // parts)
                 result = work.tile([P, D // parts], F32, name="result", bufs=5)
-                if on_pool:
-                    nc.gpsimd.tensor_scalar(out=result[:], in0=neg_v[q][:, feats], scalar1=rstd[q][:], scalar2=0.0,
-                                            op0=ALU.mult, op1=ALU.add)
-                elif on_scalar:
-                    nc.scalar.activation(out=result[:], in_=neg_v[q][:, feats], func=ACT.Copy, scale=rstd[q][:])
-                else:
-                    nc.vector.tensor_scalar(out=result[:], in0=neg_v[q][:, feats], scalar1=rstd[q][:], scalar2=None,
-                                            op0=ALU.mult)
-                nc.sync.dma_start(out=out[i].rearrange("(p h) d -> p h d", h=HALVES)[:, h, feats], in_=result[:])
+                times_rstd(result[:], v[q][:, feats], q)
+                nc.sync.dma_start(out=out[i].rearrange("(m h) d -> m h d", h=HALVES)[:, h, feats], in_=result[:])
 
-        rms, mass_bank = {}, {}
-        both = list(range(N_PASSES))
+        def when(index, step, *args):
+            if 0 <= index < UNITS:
+                step(index, *args)
 
         load_y(0, [0])
-        nc.sync.dma_start(out=w_raw[:], in_=w.rearrange("(g p t) k -> p g t k", p=P, t=PACK))
-        nc.sync.dma_start(out=scale_cols[:], in_=y_scale.rearrange("a o (g p t) -> p (a o g) t", p=P, t=PACK))
+        nc.sync.dma_start(out=scale_cols[:], in_=y_scale.rearrange("a o (g p s) -> p (a o g) s", p=P, s=PACK))
+        nc.sync.dma_start(out=w_raw[:], in_=w.rearrange("(g p s) k -> p g s k", p=P, s=PACK))
         load_y(0, [1])
         load_x(0)
-        nc.sync.dma_start(out=b_cols[:], in_=b.rearrange("(p h) -> p h", h=HALVES))
+        nc.sync.dma_start(out=b_cols[:], in_=b.rearrange("(m h) -> m h", h=HALVES))
         nc.sync.dma_start(out=t_cols[:], in_=t.rearrange("(g p s) -> p g s", p=P, s=PACK))
         load_unit(1)
-        nc.sync.dma_start(out=c_rows[:], in_=c.rearrange("(p h) d -> p h d", h=HALVES))
+        nc.sync.dma_start(out=c_rows[:], in_=c.rearrange("(m h) d -> m h d", h=HALVES))
         for u in range(2, AHEAD):
             load_unit(u)
         for g in range(E_PASSES):
-            nc.vector.tensor_copy(out=w_grouped[:, g, :, :].rearrange("p (h m) t -> p h m t", h=HALVES),
-                                  in_=w_raw[:, g, :, :].rearrange("p t (m h) -> p h m t", h=HALVES))
-
-        def quantize_w():
-            nc.vector.quantize_mx(out=w_codes[:].rearrange("p g k -> p (g k)").bitcast(FP8X4),
-                                  scales=w_scales[:].rearrange("p g k -> p (g k)"),
-                                  in_=w_grouped[:].rearrange("p g k t -> p (g k t)"))
-
-        def when(u, step, *args):
-            if 0 <= u < UNITS:
-                step(u, *args)
-
-        widen_y(0, 0)
-        turn_y(0, 0)
-        turn_y(0, 1)
-        quantize_w()
-        nc.vector.tensor_scalar(out=neg_b[:], in0=b_cols[:], scalar1=-1.0, scalar2=None, op0=ALU.mult)
+            nc.vector.tensor_copy(out=w_grouped[:, g, :, :].rearrange("p (h m) s -> p h m s", h=HALVES),
+                                  in_=w_raw[:, g, :, :].rearrange("p s (m h) -> p h m s", h=HALVES))
+        for s in range(2):
+            widen_y(0, [s])
+            turn_y(0, s)
 
         for j in range(UNITS):
-            q = j - LAG
-            widen_y(j, 1)
+            q = j - POOL_LAG
+            vector_widens = REWEIGHT_LAG <= j < POOL_LAG
+            widen_y(j, [2] if vector_widens else [2, 3])
             group_x_scalar(j)
+
             when(j - 1, quantize_y)
-            when(j - 3, row_factor)
+            if j == 1:
+                nc.vector.tensor_scalar(out=neg_b[:], in0=b_cols[:], scalar1=-1.0, scalar2=None, op0=ALU.mult)
+            when(j - REWEIGHT_LAG, row_factor)
             when(j - 1, logits)
-            when(j - 4, quantize_r)
-            when(q - 2, normalise, 1, False)
+            when(j - REWEIGHT_LAG - 1, quantize_r)
+            if vector_widens:
+                widen_y(j, [3], nc.vector.tensor_copy)
             when(j - 1, quantize_x)
-            when(q, pool_matmul, "s", both)
+
             group_x_pool(j)
-            when(j - 3, reweight_pool)
+            when(j - REWEIGHT_LAG, reweight_pool)
+            when(q - 2, normalise, times_rstd_scalar)
             when(q - 1, mean_square)
             when(q - 1, inverse_root_pow)
-            when(j - 1, add_bias, 0)
-            when(j - 1, add_bias, 1)
+            when(j - 1, add_bias)
+
             scale_y(j, 0)
+            if j == 0:
+                quantize_w()
             turn_y(j, 2)
             scale_y(j, 1)
             turn_y(j, 3)
-            when(j - 3, mass_matmul, "logit")
-            when(j - 2, row_max, 0)
-            when(j - 2, row_max, 1)
-            when(j - 2, exponentiate, 0)
-            when(j - 2, exponentiate, 1)
-            when(j - 1, turn_logits)
-            when(j + 1, widen_y, 0)
+            when(q, pool_matmul, "pool", ALL_PASSES)
+            when(j - REWEIGHT_LAG, mass_matmul)
+            when(j - 2, row_max)
+            when(j - 2, exponentiate)
+            when(j - 1, turn_logits, "soft")
+            when(j + 1, widen_y, [0, 1])
             scale_y(j, 2)
             scale_y(j, 3)
             when(j + 1, turn_y, 0)
             when(j + 1, turn_y, 1)
             when(q, centre, 0)
             when(q, centre, 1)
-            when(j - 3, mass_collect)
+            when(j - REWEIGHT_LAG, mass_collect)
             when(j - 2, invert_sums)
             if j >= 1:
                 when(j + AHEAD - 1, load_unit)
 
-        quantize_y(7)
-        row_factor(5)
-        logits(7)
-        pool_matmul(3, "s", both)
-        mean_square(2)
-        inverse_root_pow(2)
-        row_max(6, 0)
-        row_max(6, 1)
-        exponentiate(6, 0)
-        exponentiate(6, 1)
-        add_bias(7, 0)
-        add_bias(7, 1)
-        turn_logits(7)
-        mass_matmul(5, "logit")
-        quantize_r(4)
-        quantize_x(7)
-        reweight(5, nc.vector)
-        centre(3, 0)
-        centre(3, 1)
-        normalise(1, 1, True)
-        mean_square(3)
-        normalise(2, 1, True)
-        quantize_r(5)
-        invert_sums(6)
-        row_max(7, 0)
-        row_factor(6)
-        row_max(7, 1)
-        mass_collect(5)
-        exponentiate(7, 0)
-        exponentiate(7, 1)
-        root(3)
-        pool_matmul(4, "s", both)
-        pool_matmul(5, "turn", both)
-        mass_matmul(6, "logit")
-        reweight(6, nc.vector)
-        centre(4, 0)
-        quantize_r(6)
-        invert_sums(7)
-        centre(4, 1)
-        mean_square(4)
-        row_factor(7)
-        mass_collect(6)
-        root(4)
-        pool_matmul(6, "zb", [0])
-        pool_matmul(7, "s", [0])
-        mass_matmul(7, "logit")
-        reweight(7, nc.vector)
-        invert_root(3)
-        normalise(3, 1, True)
-        centre(5, 0)
-        quantize_r(7)
-        pool_matmul(6, "zb", [1])
-        pool_matmul(7, "s", [1])
-        mass_collect(7)
-        invert_root(4)
-        centre(5, 1)
-        normalise(4, 1, False, True)
-        mean_square(5)
-        centre(6, 0)
-        centre(6, 1)
-        root(5)
-        mean_square(6)
-        centre(7, 0)
-        centre(7, 1)
-        root(6)
-        mean_square(7)
-        root(7)
-        invert_root(5)
-        normalise(5)
-        invert_root(6)
-        normalise(6)
-        invert_root(7)
-        normalise(7, 2)
+        last = UNITS - 1
+
+        quantize_y(last)
+        logits(last)
+        pool_matmul(last - 4, "pool", ALL_PASSES)
+        mean_square(last - 5)
+        quantize_r(last - 3)
+        quantize_x(last)
+        row_factor(last - 2)
+        reweight_pool(last - 2)
+        inverse_root_pow(last - 5)
+        normalise(last - 6, times_rstd_scalar)
+        add_bias(last)
+        turn_logits(last, "turn")
+        mass_matmul(last - 2)
+        row_max(last - 1)
+        exponentiate(last - 1)
+        centre(last - 4, 0)
+        centre(last - 4, 1)
+        row_max(last)
+        exponentiate(last)
+        invert_sums(last - 1)
+        mass_collect(last - 2)
+
+        quantize_r(last - 2)
+        pool_matmul(last - 3, "pool", ALL_PASSES)
+        pool_matmul(last - 2, "soft", ALL_PASSES)
+        mass_matmul(last - 1)
+        row_factor(last - 1)
+        mean_square(last - 4)
+        root(last - 4)
+        reweight_vector(last - 1)
+        invert_sums(last)
+        mass_matmul(last)
+        quantize_r(last - 1)
+        row_factor(last)
+        pool_matmul(last - 1, "turn", ALL_PASSES[:1])
+        centre(last - 3, 0)
+        reweight_vector(last)
+        normalise(last - 5, times_rstd_scalar)
+        centre(last - 3, 1)
+        quantize_r(last)
+        pool_matmul(last - 1, "turn", ALL_PASSES[1:])
+        pool_matmul(last, "pool", ALL_PASSES)
+
+        mean_square(last - 3)
+        mass_collect(last - 1)
+        invert_root(last - 4)
+        normalise(last - 4, times_rstd_pool)
+        centre(last - 2, 0)
+        mass_collect(last)
+        centre(last - 2, 1)
+        root(last - 3)
+        mean_square(last - 2)
+        centre(last - 1, 0)
+        invert_root(last - 3)
+        normalise(last - 3, times_rstd_pool)
+        centre(last - 1, 1)
+        root(last - 2)
+        mean_square(last - 1)
+        centre(last, 0)
+        invert_root(last - 2)
+        normalise(last - 2, times_rstd_pool)
+        centre(last, 1)
+        root(last - 1)
+        mean_square(last)
+        root(last)
+
+        invert_root(last - 1)
+        normalise(last - 1, times_rstd_vector)
+        invert_root(last)
+        normalise(last, times_rstd_vector, 2)

@@ -36,9 +36,9 @@ NARROW_EXTRA = 128
 
 
 def pool_extra(u):
-    if u == 0 or u >= POOL_LAG:
-        return NARROW_EXTRA
-    return WIDE_EXTRA if u < REWEIGHT_LAG else 0
+    if u >= REWEIGHT_LAG:
+        return 0
+    return NARROW_EXTRA if u < 2 else WIDE_EXTRA
 
 
 def tile_crossmodalreweightedvlad_kernel(tc, y_bytes, y_scale, w, b, t, x, c, out):
@@ -101,10 +101,10 @@ def tile_crossmodalreweightedvlad_kernel(tc, y_bytes, y_scale, w, b, t, x, c, ou
                                   scales=w_scales[:].rearrange("p g k -> p (g k)"),
                                   in_=w_grouped[:].rearrange("p g k s -> p (g k s)"))
 
-        def widen_y(u, slots, copy=nc.scalar.copy):
+        def widen_y(u, slots):
             wide = work.tile([P, len(slots) * E], BF16, name="y_wide", bufs=5)
             first = slots[0] % 2 * E
-            copy(out=wide[:], in_=y_raw[u, slots[0] // 2][:, first:first + len(slots) * E].bitcast(FP8))
+            nc.scalar.copy(out=wide[:], in_=y_raw[u, slots[0] // 2][:, first:first + len(slots) * E].bitcast(FP8))
             for n, s in enumerate(slots):
                 y_wide[u, s] = wide[:].bitcast(F32)[:, n * E // 2:(n + 1) * E // 2]
 
@@ -145,19 +145,22 @@ def tile_crossmodalreweightedvlad_kernel(tc, y_bytes, y_scale, w, b, t, x, c, ou
                 nc.scalar.activation(out=neg_z[u, h][:], in_=logit_bank[u, h][:], func=ACT.Identity,
                                      bias=neg_b[:, h:h + 1], scale=-1.0)
 
-        def turn_logits(u, tag):
+        def turn_logits(u):
             for pair in range(2):
-                neg_z_turned[u, pair] = psum.tile([P, 2, K], F32, name="neg_z_turned", tag=tag)
+                neg_z_turned[u, pair] = psum.tile([P, 2, K], F32, name="neg_z_turned", tag="soft")
                 for n in range(2):
                     s = 2 * pair + n
                     for h in range(HALVES):
                         nc.tensor.transpose(neg_z_turned[u, pair][:, n, h * P:(h + 1) * P],
                                             neg_z[u, h][:, s * P:(s + 1) * P], ident[:])
 
+        def row_max_pair(u, pair):
+            neg_max[u, pair] = work.tile([P, 2], F32, name="neg_max", bufs=4)
+            nc.vector.tensor_reduce(out=neg_max[u, pair][:], in_=neg_z_turned[u, pair][:], axis=AXIS.X, op=ALU.min)
+
         def row_max(u):
             for pair in range(2):
-                neg_max[u, pair] = work.tile([P, 2], F32, name="neg_max", bufs=4)
-                nc.vector.tensor_reduce(out=neg_max[u, pair][:], in_=neg_z_turned[u, pair][:], axis=AXIS.X, op=ALU.min)
+                row_max_pair(u, pair)
 
         def exponentiate(u):
             expd[u] = work.tile([P, PACK, K], F32, name="expd", bufs=3)
@@ -290,8 +293,8 @@ def tile_crossmodalreweightedvlad_kernel(tc, y_bytes, y_scale, w, b, t, x, c, ou
                 step(index, *args)
 
         load_y(0, [0])
-        nc.sync.dma_start(out=scale_cols[:], in_=y_scale.rearrange("a o (g p s) -> p (a o g) s", p=P, s=PACK))
         nc.sync.dma_start(out=w_raw[:], in_=w.rearrange("(g p s) k -> p g s k", p=P, s=PACK))
+        nc.sync.dma_start(out=scale_cols[:], in_=y_scale.rearrange("a o (g p s) -> p (a o g) s", p=P, s=PACK))
         load_y(0, [1])
         load_x(0)
         nc.sync.dma_start(out=b_cols[:], in_=b.rearrange("(m h) -> m h", h=HALVES))
@@ -309,8 +312,7 @@ def tile_crossmodalreweightedvlad_kernel(tc, y_bytes, y_scale, w, b, t, x, c, ou
 
         for j in range(UNITS):
             q = j - POOL_LAG
-            vector_widens = REWEIGHT_LAG <= j < POOL_LAG
-            widen_y(j, [2] if vector_widens else [2, 3])
+            widen_y(j, [2, 3])
             group_x_scalar(j)
 
             when(j - 1, quantize_y)
@@ -319,13 +321,12 @@ def tile_crossmodalreweightedvlad_kernel(tc, y_bytes, y_scale, w, b, t, x, c, ou
             when(j - REWEIGHT_LAG, row_factor)
             when(j - 1, logits)
             when(j - REWEIGHT_LAG - 1, quantize_r)
-            if vector_widens:
-                widen_y(j, [3], nc.vector.tensor_copy)
+            when(q - 2, normalise, times_rstd_vector)
             when(j - 1, quantize_x)
+            when(q, pool_matmul, "pool", ALL_PASSES)
 
             group_x_pool(j)
             when(j - REWEIGHT_LAG, reweight_pool)
-            when(q - 2, normalise, times_rstd_scalar)
             when(q - 1, mean_square)
             when(q - 1, inverse_root_pow)
             when(j - 1, add_bias)
@@ -336,11 +337,10 @@ def tile_crossmodalreweightedvlad_kernel(tc, y_bytes, y_scale, w, b, t, x, c, ou
             turn_y(j, 2)
             scale_y(j, 1)
             turn_y(j, 3)
-            when(q, pool_matmul, "pool", ALL_PASSES)
             when(j - REWEIGHT_LAG, mass_matmul)
             when(j - 2, row_max)
             when(j - 2, exponentiate)
-            when(j - 1, turn_logits, "soft")
+            when(j - 1, turn_logits)
             when(j + 1, widen_y, [0, 1])
             scale_y(j, 2)
             scale_y(j, 3)
@@ -356,71 +356,75 @@ def tile_crossmodalreweightedvlad_kernel(tc, y_bytes, y_scale, w, b, t, x, c, ou
         last = UNITS - 1
 
         quantize_y(last)
+        row_factor(last - 2)
         logits(last)
         pool_matmul(last - 4, "pool", ALL_PASSES)
         mean_square(last - 5)
-        quantize_r(last - 3)
-        quantize_x(last)
-        row_factor(last - 2)
-        reweight_pool(last - 2)
         inverse_root_pow(last - 5)
-        normalise(last - 6, times_rstd_scalar)
-        add_bias(last)
-        turn_logits(last, "turn")
-        mass_matmul(last - 2)
         row_max(last - 1)
         exponentiate(last - 1)
+        add_bias(last)
+        turn_logits(last)
+        mass_matmul(last - 2)
+
+        quantize_r(last - 3)
+        quantize_x(last)
+        reweight_vector(last - 2)
         centre(last - 4, 0)
         centre(last - 4, 1)
-        row_max(last)
-        exponentiate(last)
-        invert_sums(last - 1)
-        mass_collect(last - 2)
-
-        quantize_r(last - 2)
-        pool_matmul(last - 3, "pool", ALL_PASSES)
-        pool_matmul(last - 2, "soft", ALL_PASSES)
-        mass_matmul(last - 1)
-        row_factor(last - 1)
+        normalise(last - 6, times_rstd_scalar)
         mean_square(last - 4)
-        root(last - 4)
-        reweight_vector(last - 1)
-        invert_sums(last)
-        mass_matmul(last)
-        quantize_r(last - 1)
-        row_factor(last)
-        pool_matmul(last - 1, "turn", ALL_PASSES[:1])
-        centre(last - 3, 0)
-        reweight_vector(last)
         normalise(last - 5, times_rstd_scalar)
-        centre(last - 3, 1)
-        quantize_r(last)
-        pool_matmul(last - 1, "turn", ALL_PASSES[1:])
-        pool_matmul(last, "pool", ALL_PASSES)
+        quantize_r(last - 2)
+        invert_sums(last - 1)
 
+        row_max_pair(last, 0)
+        row_factor(last - 1)
+        row_max_pair(last, 1)
+        mass_collect(last - 2)
+        exponentiate(last)
+        root(last - 4)
+        pool_matmul(last - 3, "pool", ALL_PASSES)
+        pool_matmul(last - 2, "turn", ALL_PASSES)
+        mass_matmul(last - 1)
+        reweight_vector(last - 1)
+        centre(last - 3, 0)
+        quantize_r(last - 1)
+        invert_sums(last)
+        centre(last - 3, 1)
         mean_square(last - 3)
+        row_factor(last)
         mass_collect(last - 1)
-        invert_root(last - 4)
-        normalise(last - 4, times_rstd_pool)
-        centre(last - 2, 0)
-        mass_collect(last)
-        centre(last - 2, 1)
         root(last - 3)
+
+        pool_matmul(last - 1, "soft", ALL_PASSES[:1])
+        pool_matmul(last, "pool", ALL_PASSES[:1])
+        mass_matmul(last)
+        reweight_vector(last)
+        invert_root(last - 4)
+        normalise(last - 4, times_rstd_scalar)
+        centre(last - 2, 0)
+        quantize_r(last)
+        pool_matmul(last - 1, "soft", ALL_PASSES[1:])
+        pool_matmul(last, "pool", ALL_PASSES[1:])
+        mass_collect(last)
+
+        invert_root(last - 3)
+        centre(last - 2, 1)
+        normalise(last - 3, times_rstd_pool)
         mean_square(last - 2)
         centre(last - 1, 0)
-        invert_root(last - 3)
-        normalise(last - 3, times_rstd_pool)
         centre(last - 1, 1)
         root(last - 2)
         mean_square(last - 1)
         centre(last, 0)
-        invert_root(last - 2)
-        normalise(last - 2, times_rstd_pool)
         centre(last, 1)
         root(last - 1)
         mean_square(last)
         root(last)
 
+        invert_root(last - 2)
+        normalise(last - 2, times_rstd_vector)
         invert_root(last - 1)
         normalise(last - 1, times_rstd_vector)
         invert_root(last)

from contextlib import ExitStack

import concourse.mybir as mybir
from concourse.masks import make_identity

B, N, E, K, D = 4, 1024, 1024, 256, 1024
EPS = 1e-5
FLOPS = 2 * B * N * E * K + 2 * B * N * K * D

F32 = mybir.dt.float32
BF16 = mybir.dt.bfloat16
U32 = mybir.dt.uint32
U8 = mybir.dt.uint8
FP8 = mybir.dt.float8_e4m3fn
FP8X4 = mybir.dt.float8_e4m3fn_x4
ALU = mybir.AluOpType
ACT = mybir.ActivationFunctionType
AXIS = mybir.AxisListType

P = 128
PACK = 4
PASS = P * PACK
BANK = 512
E_PASSES = E // PASS
N_PASSES = N // PASS
HALVES = K // P
UNITS = B * N_PASSES
ALL_PASSES = list(range(N_PASSES))

REWEIGHT_LAG = 3
POOL_LAG = 5
AHEAD = 4
MASS_COLS = 64
WIDE_EXTRA = 256
NARROW_EXTRA = 128


def pool_extra(u):
    if u >= REWEIGHT_LAG:
        return 0
    return NARROW_EXTRA if u < 2 else WIDE_EXTRA


def tile_crossmodalreweightedvlad_kernel(tc, y_bytes, y_scale, w, b, t, x, c, out):
    nc = tc.nc
    with ExitStack() as ctx:
        const = ctx.enter_context(tc.tile_pool(name="const", bufs=1))
        work = ctx.enter_context(tc.tile_pool(name="work", bufs=2))
        psum = ctx.enter_context(tc.psum_pool(name="psum", bufs=2))
        ctx.enter_context(tc.manual_schedule())

        ident = const.tile([P, P], F32, name="ident")
        make_identity(nc, ident[:])
        minus_half = const.tile([P, 1], F32, name="minus_half")
        nc.gpsimd.memset(minus_half[:], -0.5)
        warm_in = const.tile([P, 1], F32, name="warm_in")
        warm_out = const.tile([P, 1], F32, name="warm_out")
        nc.vector.memset(warm_in[:], 0.0)
        nc.scalar.activation(out=warm_out[:], in_=warm_in[:], func=ACT.Exp)

        scale_cols = const.tile([P, E_PASSES, PACK], F32, name="scale_cols")
        w_raw = const.tile([P, E_PASSES, PACK, K], BF16, name="w_raw")
        w_grouped = const.tile([P, E_PASSES, K, PACK], BF16, name="w_grouped", align_bytes=64)
        w_codes = const.tile([P, E_PASSES, K], U32, name="w_codes", align_bytes=64)
        w_scales = const.tile([P, E_PASSES, K], U8, name="w_scales", align_bytes=64)
        b_cols = const.tile([P, HALVES], BF16, name="b_cols")
        neg_b = const.tile([P, HALVES], F32, name="neg_b")
        t_cols = const.tile([P, N_PASSES, PACK], BF16, name="t_cols")
        c_rows = const.tile([P, HALVES, D], BF16, name="c_rows")

        y_raw, x_raw, y_wide, y_turned, y_grouped, y_q = {}, {}, {}, {}, {}, {}
        logit_bank, neg_z, neg_z_turned, neg_max, expd, sums, recip, factor = {}, {}, {}, {}, {}, {}, {}, {}
        r_grouped, r_q, x_grouped, x_q, mass_bank, neg_mass = {}, {}, {}, {}, {}, {}
        s_bank, v, mean_sq, rms, rstd = {}, {}, {}, {}, {}

        def load_y(u, pairs):
            i, g = divmod(u, N_PASSES)
            rows = work.tile([P, len(pairs) * 2 * E], U8, name="y_raw", bufs=AHEAD + 2)
            src = y_bytes[i, g * PASS:(g + 1) * PASS, :].rearrange("(p s) e -> p (s e)", s=PACK)
            nc.sync.dma_start(out=rows[:], in_=src[:, pairs[0] * 2 * E:(pairs[-1] + 1) * 2 * E])
            for n, pair in enumerate(pairs):
                y_raw[u, pair] = rows[:, n * 2 * E:(n + 1) * 2 * E]

        def load_x(u):
            i, g = divmod(u, N_PASSES)
            x_raw[u] = work.tile([P, PACK, D], BF16, name="x_raw", bufs=AHEAD)
            nc.sync.dma_start(out=x_raw[u][:], in_=x[i, g * PASS:(g + 1) * PASS, :].rearrange("(p s) d -> p s d", s=PACK))

        def load_unit(u):
            load_y(u, [0, 1])
            load_x(u)

        def quantize(name, src, width, bufs):
            codes = work.tile([P, width], U32, name=name + "_codes", bufs=bufs, align_bytes=64)
            scales = work.tile([P, width], U8, name=name + "_scales", bufs=bufs, align_bytes=64)
            nc.vector.quantize_mx(out=codes[:].bitcast(FP8X4), scales=scales[:], in_=src)
            return codes, scales

        def quantize_w():
            nc.vector.quantize_mx(out=w_codes[:].rearrange("p g k -> p (g k)").bitcast(FP8X4),
                                  scales=w_scales[:].rearrange("p g k -> p (g k)"),
                                  in_=w_grouped[:].rearrange("p g k s -> p (g k s)"))

        def widen_y(u, slots):
            wide = work.tile([P, len(slots) * E], BF16, name="y_wide", bufs=5)
            first = slots[0] % 2 * E
            nc.scalar.copy(out=wide[:], in_=y_raw[u, slots[0] // 2][:, first:first + len(slots) * E].bitcast(FP8))
            for n, s in enumerate(slots):
                y_wide[u, s] = wide[:].bitcast(F32)[:, n * E // 2:(n + 1) * E // 2]

        def turn_y(u, s):
            y_turned[u, s] = psum.tile([P, 2, E_PASSES, P], F32, name="y_turned", tag="turn")
            for g in range(E_PASSES):
                for word in range(2):
                    nc.tensor.transpose(y_turned[u, s][:, word, g, :],
                                        y_wide[u, s][:, 2 * P * g + word:2 * P * (g + 1):2], ident[:])

        def scale_y(u, s):
            if s == 0:
                y_grouped[u] = work.tile([P, E_PASSES, PACK, PASS], BF16, name="y_grouped", align_bytes=64)
            turned = y_turned[u, s][:].rearrange("p a g n -> p (a g n)").bitcast(BF16)
            nc.vector.tensor_tensor(
                out=y_grouped[u][:, :, s, :].rearrange("p g (n a e) -> p g n a e", a=2, e=2),
                in0=turned.rearrange("p (a g n e) -> p g n a e", a=2, g=E_PASSES, e=2),
                in1=scale_cols[:].rearrange("p g (a e) -> p g a e", a=2).unsqueeze(2).to_broadcast([P, E_PASSES, P, 2, 2]),
                op=ALU.mult)

        def quantize_y(u):
            y_q[u] = quantize("y", y_grouped[u][:].rearrange("p g s n -> p (g s n)"), E_PASSES * PASS, 2)

        def logits(u):
            codes, scales = y_q[u]
            for h in range(HALVES):
                logit_bank[u, h] = psum.tile([P, PASS], F32, name="logit_bank", tag="logit")
                cols = slice(h * P, (h + 1) * P)
                for g in range(E_PASSES):
                    toks = slice(g * PASS, (g + 1) * PASS)
                    nc.tensor.matmul_mx(out=logit_bank[u, h][:], lhsT=w_codes[:, g, cols].bitcast(FP8X4),
                                        lhsT_scale=w_scales[:, g, cols], rhs=codes[:, toks].bitcast(FP8X4),
                                        rhs_scale=scales[:, toks], start=(g == 0), stop=(g == E_PASSES - 1))

        def add_bias(u):
            for h in range(HALVES):
                neg_z[u, h] = work.tile([P, PASS], F32, name="neg_z", bufs=2)
                nc.scalar.activation(out=neg_z[u, h][:], in_=logit_bank[u, h][:], func=ACT.Identity,
                                     bias=neg_b[:, h:h + 1], scale=-1.0)

        def turn_logits(u):
            for pair in range(2):
                neg_z_turned[u, pair] = psum.tile([P, 2, K], F32, name="neg_z_turned", tag="soft")
                for n in range(2):
                    s = 2 * pair + n
                    for h in range(HALVES):
                        nc.tensor.transpose(neg_z_turned[u, pair][:, n, h * P:(h + 1) * P],
                                            neg_z[u, h][:, s * P:(s + 1) * P], ident[:])

        def row_max_pair(u, pair):
            neg_max[u, pair] = work.tile([P, 2], F32, name="neg_max", bufs=4)
            nc.vector.tensor_reduce(out=neg_max[u, pair][:], in_=neg_z_turned[u, pair][:], axis=AXIS.X, op=ALU.min)

        def row_max(u):
            for pair in range(2):
                row_max_pair(u, pair)

        def exponentiate(u):
            expd[u] = work.tile([P, PACK, K], F32, name="expd", bufs=3)
            sums[u] = work.tile([P, PACK], F32, name="sums")
            for s in range(PACK):
                pair, n = divmod(s, 2)
                nc.scalar.activation(out=expd[u][:, s, :], in_=neg_z_turned[u, pair][:, n, :], func=ACT.Exp,
                                     bias=neg_max[u, pair][:, n:n + 1], scale=-1.0, accum_out=sums[u][:, s:s + 1])

        def invert_sums(u):
            recip[u] = work.tile([P, PACK], F32, name="recip", bufs=3)
            nc.vector.reciprocal(out=recip[u][:], in_=sums[u][:])

        def row_factor(u):
            factor[u] = work.tile([P, PACK], F32, name="factor")
            nc.vector.tensor_tensor(out=factor[u][:], in0=recip[u][:], in1=t_cols[:, u % N_PASSES, :], op=ALU.mult)

        def reweight_vector(u):
            r_grouped[u] = work.tile([P, K, PACK], BF16, name="r_grouped", align_bytes=64)
            nc.vector.tensor_tensor(out=r_grouped[u][:].rearrange("p (k i) s -> p k s i", i=2),
                                    in0=expd[u][:].rearrange("p s (k i) -> p k s i", i=2),
                                    in1=factor[u][:].unsqueeze(1).unsqueeze(3).to_broadcast([P, K // 2, PACK, 2]),
                                    op=ALU.mult)

        def reweight_pool(u):
            r_grouped[u] = work.tile([P, K, PACK], BF16, name="r_grouped", align_bytes=64)
            nc.gpsimd.tensor_tensor(out=r_grouped[u][:], in0=expd[u][:].rearrange("p s k -> p k s"),
                                    in1=factor[u][:].unsqueeze(1).to_broadcast([P, K, PACK]), op=ALU.mult)

        def quantize_r(u):
            r_q[u] = quantize("r", r_grouped[u][:].rearrange("p k s -> p (k s)"), K, POOL_LAG)

        def pool_copy(u, dh, cols):
            nc.gpsimd.tensor_scalar(out=x_grouped[u, dh][:, :cols, :],
                                    in0=x_raw[u][:, :, dh * BANK:dh * BANK + cols].rearrange("p s d -> p d s"),
                                    scalar1=1.0, scalar2=0.0, op0=ALU.mult, op1=ALU.add)

        def group_x_pool(u):
            x_grouped[u, 0] = work.tile([P, BANK, PACK], BF16, name="x_grouped", tag="x_pool", bufs=1, align_bytes=64)
            pool_copy(u, 0, BANK)
            if pool_extra(u):
                pool_copy(u, 1, pool_extra(u))

        def group_x_scalar(u):
            x_grouped[u, 1] = work.tile([P, BANK, PACK], BF16, name="x_grouped", tag="x_scalar", align_bytes=64)
            nc.scalar.copy(out=x_grouped[u, 1][:, pool_extra(u):, :].rearrange("p (d i) s -> p d s i", i=4),
                           in_=x_raw[u][:, :, BANK + pool_extra(u):].rearrange("p s (d i) -> p d s i", i=4))

        def quantize_x(u):
            for dh in (1, 0):
                x_q[u, dh] = quantize("x", x_grouped[u, dh][:].rearrange("p d s -> p (d s)"), BANK, 2 * (POOL_LAG + 1))

        def mass_matmul(u):
            mass_bank[u] = psum.tile([P, HALVES, MASS_COLS], F32, name="mass_bank", tag="logit")
            for h in range(HALVES):
                for s in range(PACK):
                    nc.tensor.matmul(mass_bank[u][:, h, :], lhsT=expd[u][:, s, h * P:(h + 1) * P],
                                     rhs=recip[u][:, s:s + 1].to_broadcast([P, MASS_COLS]),
                                     start=(s == 0), stop=(s == PACK - 1))

        def mass_collect(u):
            neg_mass[u] = work.tile([P, HALVES], F32, name="neg_mass", bufs=UNITS)
            if u % N_PASSES == 0:
                nc.vector.tensor_scalar(out=neg_mass[u][:], in0=mass_bank[u][:, :, 0], scalar1=-1.0, scalar2=None,
                                        op0=ALU.mult)
            else:
                nc.vector.tensor_tensor(out=neg_mass[u][:], in0=neg_mass[u - 1][:], in1=mass_bank[u][:, :, 0],
                                        op=ALU.subtract)

        def pool_matmul(q, tag, passes):
            i, h = divmod(q, HALVES)
            cols = slice(h * P, (h + 1) * P)
            for dh in range(D // BANK):
                if passes[0] == 0:
                    s_bank[q, dh] = psum.tile([P, BANK], F32, name="s_bank", tag=tag)
                for g in passes:
                    r_codes, r_scales = r_q[N_PASSES * i + g]
                    x_codes, x_scales = x_q[N_PASSES * i + g, dh]
                    nc.tensor.matmul_mx(out=s_bank[q, dh][:], lhsT=r_codes[:, cols].bitcast(FP8X4),
                                        lhsT_scale=r_scales[:, cols], rhs=x_codes[:].bitcast(FP8X4),
                                        rhs_scale=x_scales[:], start=(g == 0), stop=(g == N_PASSES - 1))

        def centre(q, dh):
            i, h = divmod(q, HALVES)
            if dh == 0:
                v[q] = work.tile([P, D], F32, name="v", bufs=5)
            feats = slice(dh * BANK, (dh + 1) * BANK)
            nc.vector.scalar_tensor_tensor(out=v[q][:, feats], in0=c_rows[:, h, feats],
                                           scalar=neg_mass[N_PASSES * (i + 1) - 1][:, h:h + 1],
                                           in1=s_bank[q, dh][:], op0=ALU.mult, op1=ALU.add)

        def mean_square(q):
            squares = work.tile([P, D], BF16, name="squares", bufs=2)
            mean_sq[q] = work.tile([P, 1], F32, name="mean_sq", bufs=4)
            nc.scalar.activation(out=squares[:], in_=v[q][:], func=ACT.Square, scale=D ** -0.5, accum_out=mean_sq[q][:])

        def inverse_root_pow(q):
            shifted = work.tile([P, 1], F32, name="shifted")
            rstd[q] = work.tile([P, 1], F32, name="rstd", bufs=4)
            nc.gpsimd.tensor_scalar(out=shifted[:], in0=mean_sq[q][:], scalar1=EPS, scalar2=1.0, op0=ALU.add, op1=ALU.mult)
            nc.gpsimd.tensor_tensor(out=rstd[q][:], in0=shifted[:], in1=minus_half[:], op=ALU.pow)

        def root(q):
            rms[q] = work.tile([P, 1], F32, name="rms", bufs=4)
            nc.scalar.activation(out=rms[q][:], in_=mean_sq[q][:], func=ACT.Sqrt, bias=EPS)

        def invert_root(q):
            rstd[q] = work.tile([P, 1], F32, name="rstd_tail", bufs=4)
            nc.vector.reciprocal(out=rstd[q][:], in_=rms[q][:])

        def times_rstd_scalar(dst, src, q):
            nc.scalar.activation(out=dst, in_=src, func=ACT.Copy, scale=rstd[q][:])

        def times_rstd_pool(dst, src, q):
            nc.gpsimd.tensor_scalar(out=dst, in0=src, scalar1=rstd[q][:], scalar2=0.0, op0=ALU.mult, op1=ALU.add)

        def times_rstd_vector(dst, src, q):
            nc.vector.tensor_scalar(out=dst, in0=src, scalar1=rstd[q][:], scalar2=None, op0=ALU.mult)

        def normalise(q, times_rstd, parts=1):
            i, h = divmod(q, HALVES)
            for part in range(parts):
                feats = slice(part * D // parts, (part + 1) * D // parts)
                result = work.tile([P, D // parts], F32, name="result", bufs=5)
                times_rstd(result[:], v[q][:, feats], q)
                nc.sync.dma_start(out=out[i].rearrange("(m h) d -> m h d", h=HALVES)[:, h, feats], in_=result[:])

        def when(index, step, *args):
            if 0 <= index < UNITS:
                step(index, *args)

        load_y(0, [0])
        nc.sync.dma_start(out=w_raw[:], in_=w.rearrange("(g p s) k -> p g s k", p=P, s=PACK))
        nc.sync.dma_start(out=scale_cols[:], in_=y_scale.rearrange("a o (g p s) -> p (a o g) s", p=P, s=PACK))
        load_y(0, [1])
        load_x(0)
        nc.sync.dma_start(out=b_cols[:], in_=b.rearrange("(m h) -> m h", h=HALVES))
        nc.sync.dma_start(out=t_cols[:], in_=t.rearrange("(g p s) -> p g s", p=P, s=PACK))
        load_unit(1)
        nc.sync.dma_start(out=c_rows[:], in_=c.rearrange("(m h) d -> m h d", h=HALVES))
        for u in range(2, AHEAD):
            load_unit(u)
        for g in range(E_PASSES):
            nc.vector.tensor_copy(out=w_grouped[:, g, :, :].rearrange("p (h m) s -> p h m s", h=HALVES),
                                  in_=w_raw[:, g, :, :].rearrange("p s (m h) -> p h m s", h=HALVES))
        for s in range(2):
            widen_y(0, [s])
            turn_y(0, s)

        for j in range(UNITS):
            q = j - POOL_LAG
            widen_y(j, [2, 3])
            group_x_scalar(j)

            when(j - 1, quantize_y)
            if j == 1:
                nc.vector.tensor_scalar(out=neg_b[:], in0=b_cols[:], scalar1=-1.0, scalar2=None, op0=ALU.mult)
            when(j - REWEIGHT_LAG, row_factor)
            when(j - 1, logits)
            when(j - REWEIGHT_LAG - 1, quantize_r)
            when(q - 2, normalise, times_rstd_vector)
            when(j - 1, quantize_x)
            when(q, pool_matmul, "pool", ALL_PASSES)

            group_x_pool(j)
            when(j - REWEIGHT_LAG, reweight_pool)
            when(q - 1, mean_square)
            when(q - 1, inverse_root_pow)
            when(j - 1, add_bias)

            scale_y(j, 0)
            if j == 0:
                quantize_w()
            turn_y(j, 2)
            scale_y(j, 1)
            turn_y(j, 3)
            when(j - REWEIGHT_LAG, mass_matmul)
            when(j - 2, row_max)
            when(j - 2, exponentiate)
            when(j - 1, turn_logits)
            when(j + 1, widen_y, [0, 1])
            scale_y(j, 2)
            scale_y(j, 3)
            when(j + 1, turn_y, 0)
            when(j + 1, turn_y, 1)
            when(q, centre, 0)
            when(q, centre, 1)
            when(j - REWEIGHT_LAG, mass_collect)
            when(j - 2, invert_sums)
            if j >= 1:
                when(j + AHEAD - 1, load_unit)

        last = UNITS - 1

        quantize_y(last)
        row_factor(last - 2)
        logits(last)
        pool_matmul(last - 4, "pool", ALL_PASSES)
        mean_square(last - 5)
        inverse_root_pow(last - 5)
        row_max(last - 1)
        exponentiate(last - 1)
        add_bias(last)
        turn_logits(last)
        mass_matmul(last - 2)

        quantize_r(last - 3)
        quantize_x(last)
        reweight_vector(last - 2)
        centre(last - 4, 0)
        centre(last - 4, 1)
        normalise(last - 6, times_rstd_scalar)
        mean_square(last - 4)
        normalise(last - 5, times_rstd_scalar)
        quantize_r(last - 2)
        invert_sums(last - 1)

        row_max_pair(last, 0)
        row_factor(last - 1)
        row_max_pair(last, 1)
        mass_collect(last - 2)
        exponentiate(last)
        root(last - 4)
        pool_matmul(last - 3, "pool", ALL_PASSES)
        pool_matmul(last - 2, "turn", ALL_PASSES)
        mass_matmul(last - 1)
        reweight_vector(last - 1)
        centre(last - 3, 0)
        quantize_r(last - 1)
        invert_sums(last)
        centre(last - 3, 1)
        mean_square(last - 3)
        row_factor(last)
        mass_collect(last - 1)
        root(last - 3)

        pool_matmul(last - 1, "soft", ALL_PASSES[:1])
        pool_matmul(last, "pool", ALL_PASSES[:1])
        mass_matmul(last)
        reweight_vector(last)
        invert_root(last - 4)
        normalise(last - 4, times_rstd_scalar)
        centre(last - 2, 0)
        quantize_r(last)
        pool_matmul(last - 1, "soft", ALL_PASSES[1:])
        pool_matmul(last, "pool", ALL_PASSES[1:])
        mass_collect(last)

        invert_root(last - 3)
        centre(last - 2, 1)
        normalise(last - 3, times_rstd_pool)
        mean_square(last - 2)
        centre(last - 1, 0)
        centre(last - 1, 1)
        root(last - 2)
        mean_square(last - 1)
        centre(last, 0)
        centre(last, 1)
        root(last - 1)
        mean_square(last)
        root(last)

        invert_root(last - 2)
        normalise(last - 2, times_rstd_vector)
        invert_root(last - 1)
        normalise(last - 1, times_rstd_vector)
        invert_root(last)
        normalise(last, times_rstd_vector, 2)
